import numpy as np, ml_dtypes
CORES = [24,25,26,27,28,29,30,31]
N = 8
BF = ml_dtypes.bfloat16
H, P, B, T, S = 4096, 1536, 128, 4, 32
BOUND = P + B * (np.arange(T * B) // B)
def parts(rng):
    G = P + T * B
    fe = (256 * (0.6 * rng.random((N, 8, 16, G)) + 0.4 * rng.random((N, 8, 1, G)))).astype(np.int64)
    no = (256 * (0.6 * rng.random((N, 8, 16, H)) + 0.4 * rng.random((N, 8, 1, H)))).astype(np.int64)
    no = np.minimum(no + rng.integers(0, 64, (N, 8, 1, 1)), 255)
    co = rng.integers(0, BOUND, (N, 8, 16, T * B))
    pool = np.argsort(rng.random((N, 8, H)), axis=-1)[..., :256]; ix = (256 * rng.random((N, 8, P)) ** 3).astype(np.int64)
    hv = np.where(rng.random((N, 8, P)) < 0.3, rng.integers(0, H, (N, 8, P)), np.take_along_axis(pool, ix, 2))
    return fe, no, co, hv
def pack(fe, no, co, hv):
    return {"lim": np.ascontiguousarray(no.reshape(N, 128, H)).astype(np.float32).astype(BF), "feat": np.ascontiguousarray(fe.reshape(N, 128, P + T * B)).astype(np.float32).astype(BF),
            "comp": np.ascontiguousarray(co.reshape(N, 128, T * B)).astype(np.int32), "hd": np.ascontiguousarray(hv).astype(np.int32)}
def setup_inputs(rng):
    return pack(*parts(rng))
def setup_inputs_ties(rng):
    fe, no, co, hv = parts(rng)
    d = rng.permutation(np.array([1, 2, S - 1, S, S + 1, S, 1, S + 1])).reshape(1, 8, 1, 1)
    fe = 100 + d * (rng.random(fe.shape) < 0.8).astype(np.int64); no = 100 + d * (rng.random(no.shape) < 0.35).astype(np.int64)
    fe[..., 1::2] = fe[..., 0::2].copy()
    co[:, :, 8:, ::3] = co[:, :, :8, ::3].copy()
    return pack(fe, no, co, hv)
def setup_inputs_alike(rng):
    fe, no, co, hv = parts(rng)
    hv[:, ::2] = rng.choice(np.array([0, H - 1, H // 2, 37]), (N, 4, P)); hv[..., 0] = H - 1; hv[..., P - 1] = 0
    no[:, :4] = rng.integers(200, 256, (N, 4, 16, H))
    co[:, 1] = co[:, 1, :1].copy()
    co[:, 3] = np.where(rng.random((N, 16, T * B)) < 0.5, 0, BOUND - 1)
    co[:, 5] = rng.integers(BOUND - B, BOUND, (N, 16, T * B))
    co[:, 7, 2:] = np.where(rng.random((N, 14, T * B)) < 0.5, co[:, 7, :1], co[:, 7, 1:2])
    return pack(fe, no, co, hv)
def setup_inputs_ends(rng):
    fe, no, co, hv = parts(rng); M = T * B; k = np.arange(16)[:, None]
    for g in range(5): hv[:, g] = rng.permutation(H)[:P]
    no[:, :5] = 255
    o = np.argsort(rng.random((N, 16, M)), axis=1); s = rng.integers(0, P // 2, (N, 1, M))
    fe[:, 0] = 255; fe[:, 0, :, 1:P:2] = 0
    co[:, 0] = np.where(o < 2, 2 * rng.integers(0, P // 2, (N, 1, M)) + 1, 2 * ((s + o) % (P // 2)))
    fe[:, 1, :, :P] = rng.integers(200, 256, (N, 16, P)); fe[:, 1, :, P:] = 255
    lo = np.argsort(rng.random((N, 3, T, B)), axis=-1)
    lo[:, 1:] = 0; lo[:, 2, :, 1:-1] = 1 + np.argsort(rng.random((N, T, B - 1)), axis=-1)[..., :B - 2]
    w = B + rng.integers(0, P - B, (N, 3, 1, M))
    co[:, 2:5] = np.where(k == rng.integers(0, 16, (N, 3, 1, M)), lo.reshape(N, 3, 1, M), w)
    fe[:, 2:5, :, P:] = rng.integers(0, 160, (N, 3, 16, M)); fe[:, 4, :, P::B] = 255
    for g, b in ((5, 254), (6, 0)):
        fe[:, g] = b + (rng.random((N, 16, P + M)) < 0.8).astype(np.int64); no[:, g] = b + (rng.random((N, 16, H)) < 0.3).astype(np.int64)
    return pack(fe, no, co, hv)
def setup_inputs_still(rng):
    fe, no, co, hv = parts(rng); fe = np.maximum(fe, 1)
    z = rng.integers(0, 3, (N, 8, 1, 1)); z[:, 0] = 0; z[:, 1] = 1; z[:, 2] = 2
    return pack(fe, np.where(z == 0, 255, np.where(z == 1, 0, no)), co, hv)
def setup_inputs_spread(rng):
    fe, no, co, hv = parts(rng)
    fe = (np.exp2(8 * rng.random((N, 8, 1, P + T * B))) * rng.random(fe.shape)).astype(np.int64)
    no = (np.exp2(8 * rng.random((N, 8, 1, H))) * rng.random(no.shape)).astype(np.int64)
    hv = (H * rng.random((N, 8, P)) ** 4).astype(np.int64)
    return pack(fe, no, co, hv)
def check_inputs(d):
    bad = []
    for k in ("lim", "feat"):
        x = np.asarray(d[k]).astype(np.float32)
        if not np.all((x >= 0) & (x <= 255) & (x == np.floor(x))): bad.append("whole numbers of " + k)
    if np.min(d["hd"]) < 0 or np.max(d["hd"]) > H - 1: bad.append("range of hd")
    if np.min(d["comp"]) < 0 or not np.all(np.asarray(d["comp"]) < BOUND): bad.append("range of comp")
    return bad
def reference(lim, feat, comp, hd):
    fe = feat.astype(np.float32).astype(np.int16).reshape(N, 8, 16, P + T * B); no = lim.astype(np.float32).astype(np.int16).reshape(N, 8, 16, H)
    co = comp.astype(np.int64).reshape(N, 8, 16, T * B)
    h = np.zeros((N, 8, P + T * B), np.int64); h[:, :, :P] = hd
    kappa = np.zeros(N, np.int64); ranks = np.arange(N)
    for t in range(T):
        fv = fe[..., P + t * B:P + (t + 1) * B]
        ix = co[..., t * B:(t + 1) * B].reshape(N, 8, 16 * B)
        c = np.take_along_axis(h, ix, 2)
        fc = np.take_along_axis(fe, ix[:, :, None, :], 3).reshape(N, 8, 16, 16, B)
        share = np.add.reduce(np.minimum(fv[:, :, :, None, :], fc), axis=2, dtype=np.int64)
        for a in range(N):
            q = (ranks + a) % N
            x = np.take_along_axis(no[q], c[:, :, None, :], 3).reshape(N, 8, 16, 16, B)
            n = np.add.reduce(fv[:, :, :, None, :] > x, axis=2, dtype=np.int64).reshape(N, 8, 16 * B)
            c = np.where(n >= 9, ((c * c >> 5) + c + 613 * n + kappa[q][:, None, None]) & (H - 1), c)
        c = c.reshape(N, 8, 16, B)
        m = np.add.reduce(c[:, :, :, None, :] == c[:, :, None, :, :], axis=3, dtype=np.int64)
        key = 4096 * m + share
        won = np.take_along_axis(c, np.argmax(key, axis=2)[:, :, None, :], 2)[:, :, 0]
        lost = np.take_along_axis(c, np.argmin(key, axis=2)[:, :, None, :], 2)[:, :, 0]
        h[:, :, P + t * B:P + (t + 1) * B] = won
        for r in range(N):
            for g in range(8):
                e, first = np.unique(lost[r, g], return_index=True)
                old = no[r, g][:, e]
                no[r, g][:, e] = old + np.clip(fv[r, g][:, first] - old, -S, S)
        kappa = np.add.reduce(won, axis=(1, 2)) & 255
    return {"yh": h[:, :, P:].astype(np.float32), "yl": no.reshape(N, 128, H).astype(np.float32).astype(BF)}

@@ -1,0 +1,542 @@
+from concourse.bass import DstId, RemoteDMATransfer
+from concourse.mybir import AluOpType as OP, AxisListType, ActivationFunctionType as AF
+
+N = 8
+H, P0, B, ROUNDS = 4096, 1536, 128, 4
+SL = H + B
+W = 613 + 4096 * 129
+R = (9 * W // 4096) * 4096
+SUBS = ((576, 1024), (0, 256), (256, 448), (448, 576))
+SHARE_AT = 4
+MS = 144
+
+SCRATCH = {
+    "notes": ("sbuf", [128, N * SL], "bfloat16"),
+    "yy": ("sbuf", [128, 16, 128], "float16"),
+    "cf": ("sbuf", [128, 512], "float16"),
+    "dt": ("sbuf", [128, 8, 16], "bfloat16"),
+    "eq": ("sbuf", [128, 8, 128], "bfloat16"),
+    "val": ("sbuf", [128, 2, 8], "int32"),
+}
+for _d, _l in (("bfloat16", (("fe", 2048), ("hw", 2048), ("cnt", 2048), ("hdb", 192), ("dm", 256), ("blk", 128), ("vv", 128), ("vt", 128), ("idn", 128),
+                             ("idm", 128), ("idb", 128), ("ones", 128), ("xo", 128), ("xc", 128), ("hlb", 16), ("xx", 512))),
+               ("int32", (("ci0", 512), ("hdi", 96), ("hdx", 192), ("ia", 128), ("ib", 128), ("ja", 128), ("jb", 128), ("ka", 128), ("kb", 128), ("iq", 32),
+                          ("ix", 4), ("imd", 8), ("hl", 32), ("d2", 8), ("ki", 1), ("kj", 1))),
+               ("uint16", (("offq", 32), ("offx", 4), ("loff", 8), ("offc", 128 * ROUNDS))),
+               ("float32", (("md", 8), ("kc1", 64), ("kc2", 64), ("lv", 8), ("dd", 8), ("d1", 8), ("xn", 128), ("con", 2), ("ks", 1), ("yhs", 512)))):
+    for _n, _w in _l:
+        SCRATCH[_n] = ("sbuf", [128, _w], _d)
+for _h in range(2):
+    for _n, _w, _d in (("gx", 1024, "bfloat16"), ("cm", 1024, "bfloat16"), ("gs", 1024, "bfloat16"), ("cs", 1024, "bfloat16"), ("fvs", 512, "bfloat16"),
+                       ("off", 64, "uint16"), ("ci", 128, "int32"), ("cc", 64, "float32"), ("sq", 64, "float32"), ("vs", 64, "int32"),
+                       ("rr", 64, "float32"), ("qi", 64, "int32"), ("st", 64, "float32"), ("shw", 64, "float32"),
+                       ("shl", 64, "float32"), ("mx", 16, "float32")):
+        SCRATCH[_n + "_%d" % _h] = ("sbuf", [128, _w], _d)
+    SCRATCH["ee_%d" % _h] = ("sbuf", [128, 8, 96], "bfloat16")
+    for _n, _w in (("kk", 64), ("t1", 32), ("t2", 16), ("t3", 8), ("oh", 64), ("pp", 64)):
+        SCRATCH[_n + "_%d" % _h] = ("sbuf", [128, 2, _w], "float32")
+    for _n in ("fvx", "nn", "el", "au"):
+        SCRATCH[_n + "_%d" % _h] = ("psum", [128, 512], "float32")
+for _t in range(ROUNDS - 1):
+    SCRATCH["msg%d" % _t] = ("sbuf", [128, MS], "uint16")
+    SCRATCH["inb%d" % _t] = ("sbuf", [128, N * MS], "uint16")
+    SCRATCH["kap%d" % (_t + 1)] = ("sbuf", [128, N], "float32")
+
+DMAS = ["comp0", "comp1", "hd", "fe0", "fe1", "lim", "hwa", "hwb", "yh0", "yh1", "yh2", "yh3", "yl"]
+SEMAPHORES = (["pV", "pA", "pP", "pG", "lsem", "msem"] + ["d_" + n for n in DMAS] + ["lim%d" % q for q in range(N)]
+              + ["m%d_%d" % (t, q) for t in range(ROUNDS - 1) for q in range(N)])
+
+CY = 1.0
+HOP = 80.0
+
+
+def build(g, r, T, topo):
+    ops = []
+    hist = {}
+    banks = {}
+    core = T.cores[r]
+    V, A, PE, S = g.vector, g.scalar, g.tensor, g.sync
+
+    def add(eng, kind, fns, reads, writes, dur, name=None, extra=()):
+        i = len(ops)
+        deps = {}
+        for u in extra:
+            deps[u] = True
+        for buf, lo, hi in reads:
+            for acc in hist.get(buf, ()):
+                if acc[3] and acc[1] < hi and lo < acc[2]:
+                    deps[acc[0]] = True
+        for buf, lo, hi in writes:
+            for acc in hist.get(buf, ()):
+                if acc[1] < hi and lo < acc[2]:
+                    deps.setdefault(acc[0], False)
+        for buf in sorted({x[0] for x in list(reads) + list(writes)}):
+            if SCRATCH.get(buf, ("",))[0] == "psum":
+                last = banks.setdefault(buf, {})
+                for e, u in last.items():
+                    if e != eng:
+                        deps[u] = True
+                last[eng] = i
+        for buf, lo, hi in writes:
+            h = [a for a in hist.get(buf, []) if not (lo <= a[1] and a[2] <= hi)]
+            h.append((i, lo, hi, True))
+            hist[buf] = h
+        for buf, lo, hi in reads:
+            hist.setdefault(buf, []).append((i, lo, hi, False))
+        deps.pop(i, None)
+        ops.append({"e": eng, "k": kind, "f": fns, "d": deps, "t": dur, "n": name})
+        return i
+
+    def o(name, lo, hi):
+        return (T[name][:, lo:hi], (name, lo, hi))
+
+    def cyc(n, *ops2):
+        both = all(SCRATCH.get(x[1][0], ("",))[0] == "sbuf" for x in ops2)
+        return max(64, n * (2 if both and len(ops2) == 2 else 1)) * CY
+
+    def vtt(out, a, b, op, n):
+        return add("V", "c", [lambda: V.tensor_tensor(out[0], a[0], b[0], op)], [a[1], b[1]], [out[1]], cyc(n, a, b))
+
+    def vts(out, a, s1, op, n, s2=None, op1=None, sreg=None, half=False):
+        def f():
+            if op1 is None:
+                return V.tensor_scalar(out[0], a[0], s1, None, op)
+            return V.tensor_scalar(out[0], a[0], s1, s2, op, op1)
+        return add("V", "c", [f], [a[1]] + ([sreg] if sreg else []), [out[1]], max(64, n * (0.5 if half else 1)) * CY)
+
+    def vcp(out, a, n):
+        return add("V", "c", [lambda: V.tensor_copy(out[0], a[0])], [a[1]], [out[1]], max(64, n) * CY)
+
+    def fill(name, lo, hi, x, dur=64.0):
+        return add("V", "c", [lambda: V.memset(T[name][:, lo:hi], x)], [], [(name, lo, hi)], dur)
+
+    def acp(out, a, n, func=AF.Copy, **kw):
+        return add("A", "c", [lambda: A.activation(out[0], a[0], func, **kw)], [a[1]] + ([("con", 0, 2)] if kw else []), [out[1]], 65 + n * CY)
+
+    def agather(out, win, offs, n):
+        return add("A", "c", [lambda: A.activation(out[0], win[0].indirect(offs[0]), AF.Copy)], [win[1], offs[1]], [out[1]], 65 + n * 1.5 * CY)
+
+    def vgtt(out, win, offs, b, op, n):
+        return add("V", "c", [lambda: V.tensor_tensor(out[0], win[0].indirect(offs[0]), b[0], op)], [win[1], offs[1], b[1]], [out[1]], 50 + n * 1.5 * CY)
+
+    def mms(out, pairs, n):
+        last = len(pairs) - 1
+        fns = [(lambda l=l, x=x, i=i: PE.matmul(out[0], l[0], x[0], i == 0, i == last)) for i, (l, x) in enumerate(pairs)]
+        return add("P", "c", fns, sorted({x[1] for p in pairs for x in p}), [out[1]], len(pairs) * max(64, n) * 0.85 * CY)
+
+    def dma(q, name, out, in_, reads, writes, dur=2500.0):
+        eng = {"S": S, "A": A}[q]
+        return add(q, "d", [lambda: eng.dma_start(out, in_)], reads, writes, dur, name)
+
+    def cnt(a):
+        return o("cnt", 128 * a, 128 * a + 128)
+
+    def count(out, buf):
+        x = T[buf]
+        return mms(out, [(cnt(a), (x[:, a:1024:16], (buf, 0, 1024))) for a in range(16)], 64)
+
+    dma("A", "lim", T.notes[:, r * SL:r * SL + H], T.lim[:], [], [("notes", r * SL, r * SL + H)], 5000.0)
+    dma("S", "comp0", T.ci0[:, 0:128], T.comp[:, 0:128], [], [("ci0", 0, 128)])
+    dma("S", "hd", T.hdi[:], T.hd[:], [], [("hdi", 0, 96)])
+    dma("S", "fe1", T.fe[:, P0:2048], T.feat[:, P0:2048], [], [("fe", P0, 2048)])
+    dma("S", "fe0", T.fe[:, 0:P0], T.feat[:, 0:P0], [], [("fe", 0, P0)], 4000.0)
+    dma("S", "comp1", T.ci0[:, 128:512], T.comp[:, 128:512], [], [("ci0", 128, 512)])
+
+    def iota(name, w, pat, base, ch):
+        out = T[name]
+        kw = {} if SCRATCH[name][2] == "int32" else {"allow_small_or_imprecise_dtypes": True}
+        add("G", "c", [lambda: g.iota(out[:, 0:w], pat, base, ch, **kw)], [], [(name, 0, w)], 130 + 2 * w)
+    iota("ia", 128, [[0, 128]], 0, 1)
+    iota("ib", 128, [[1, 128]], 0, 0)
+    iota("iq", 32, [[1, 32]], 0, 0)
+    iota("imd", 8, [[16, 8]], H, 0)
+    iota("kc1", 64, [[-1, 16], [0, 4]], 15, 0)
+    iota("kc2", 64, [[-1, 16], [0, 4]], 0, 0)
+    w128 = lambda n: o(n, 0, 128)
+    fill("con", 0, 1, 16.0)
+    fill("con", 1, 2, float(R))
+    zeros = fill("hw", 0, 2048, 0.0, 1024.0)
+    vts(w128("ja"), w128("ia"), 4, OP.arith_shift_right, 128)
+    vts(w128("jb"), w128("ib"), 4, OP.arith_shift_right, 128)
+    vts(w128("ka"), w128("ia"), 15, OP.bitwise_and, 128)
+    vts(w128("kb"), w128("ib"), 15, OP.bitwise_and, 128)
+    vtt(w128("blk"), w128("ja"), w128("jb"), OP.is_equal, 128)
+    vtt(w128("dm"), w128("ka"), w128("kb"), OP.is_equal, 128)
+    vcp(o("dm", 128, 256), w128("dm"), 64)
+    vts(w128("vt"), w128("blk"), -99.0, OP.mult, 128, 99.0, OP.add, half=True)
+    vtt(w128("vv"), w128("vt"), w128("kb"), OP.add, 128)
+    vtt(w128("idn"), w128("blk"), w128("dm"), OP.mult, 128)
+    vts(w128("idm"), w128("idn"), -1.0, OP.mult, 128, half=True)
+
+    vts(o("hdx", 0, 96), o("hdi", 0, 96), 4032, OP.bitwise_and, 96)
+    vts(o("hdx", 96, 192), o("hdi", 0, 96), 63, OP.bitwise_and, 96)
+    vcp(o("hdb", 0, 192), o("hdx", 0, 192), 192)
+    dma("S", "hwa", T.hw[0:128:16, 0:P0], T.hdb[:, 0:96], [("hdb", 0, 96)], [("hw", 0, P0)])
+    keep = list(hist["hw"])
+    hist["hw"] = []
+    i2 = dma("S", "hwb", T.hw[1:128:16, 0:P0], T.hdb[:, 96:192], [("hdb", 96, 192)], [("hw", 0, P0)])
+    ops[i2]["d"][zeros] = True
+    hist["hw"] = keep + [(i2, 0, P0, True)]
+    for a in range(16):
+        vts(cnt(a), w128("vv"), float(a), OP.is_equal, 128, half=True)
+
+    def convert(t):
+        c0 = 128 * t
+        vcp(o("cf", c0, c0 + 128), o("ci0", c0, c0 + 128), 128)
+        for k in range(16):
+            vts((T.yy[:, k, :], ("yy", 128 * k, 128 * k + 128)), o("cf", c0, c0 + 128), T.dm[:, k:k + 1], OP.mult, 128, sreg=("dm", 0, 128), half=True)
+        for h in range(2):
+            out = o("au_%d" % h, 256, 320)
+            mms(out, [(cnt(a), (T.yy[:, :, 64 * h + a:64 * h + 64:16], ("yy", 0, 2048))) for a in range(16)], 64)
+            vcp(o("offc", 128 * t + 64 * h, 128 * t + 64 * h + 64), out, 64)
+
+    convert(0)
+    for a in range(1, N):
+        dst = T.cores[(r - a) % N]
+
+        def fn(dst=dst):
+            rid, pid = topo.addr(dst)[:2]
+            return g.remote_dma(T.notes[:, r * SL:r * SL + H], T.notes[:, r * SL:r * SL + H], T.sem["lim%d" % r], T.sem.lsem, pid, rid, topo.mask(core, dst))
+        sent = add("G", "r", [fn], [("notes", r * SL, r * SL + H)], [], 1000.0, name=("lsem", len(topo.engines(core, dst))))
+        q = (r + a) % N
+        add("X", "a", [], [], [("notes", q * SL, q * SL + H)], 4000.0, ("lim%d" % q, len(topo.engines(T.cores[q], core))), extra=[sent])
+
+    def tables():
+        vts(w128("idb"), w128("idn"), 65536.0, OP.mult, 128, half=True)
+        fill("ones", 0, 128, 1.0)
+        vcp(o("offq", 0, 32), o("iq", 0, 32), 32)
+        vts(o("ix", 0, 4), o("ia", 0, 4), 3, OP.bitwise_and, 4)
+        vcp(o("offx", 0, 4), o("ix", 0, 4), 4)
+        vtt(o("md", 0, 8), o("imd", 0, 8), o("ka", 0, 8), OP.add, 8)
+        for b in range(8):
+            vtt((T.dt[:, b, :], ("dt", 16 * b, 16 * b + 16)), o("kb", 0, 16), o("ka", 0, 16), OP.is_lt, 16)
+
+    def fvx(t, h):
+        c0 = P0 + 128 * t + 64 * h
+        x = o("fe", c0, c0 + 64)
+        name = "fvx_%d" % h
+        fns = [(lambda j=j: PE.matmul(T[name][:, 64 * j:64 * j + 64], T.idn[:], x[0], True, True)) for j in range(8)]
+        add("P", "c", fns, [("idn", 0, 128), x[1]], [(name, 0, 512)], 8 * 64 * 0.85)
+        w = SUBS[0][1] - SUBS[0][0]
+        acp(o("fvs_%d" % h, 0, w), o(name, 0, w), w)
+
+    def heads(t, h):
+        oc = 128 * t + 64 * h
+        for s in range(2):
+            agather(o("gx_%d" % h, 512 * s, 512 * s + 512), o("hw", 0, 2048), o("offc", oc + 32 * s, oc + 32 * s + 32), 512)
+        out = o("au_%d" % h, 0, 64)
+        count(out, "gx_%d" % h)
+        vcp(o("off_%d" % h, 0, 64), out, 64)
+        acp(o("cc_%d" % h, 0, 64), out, 64)
+
+    def shares(t, h):
+        oc = 128 * t + 64 * h
+        c0 = P0 + 128 * t + 64 * h
+        x, el, d = T.fe[:, c0:c0 + 64], T["el_%d" % h], o("el_%d" % h, 0, 512)
+        for s in range(2):
+            c = (512 * s, 512 * s + 512)
+            agather(o("gs_%d" % h, *c), o("fe", 0, 2048), o("offc", oc + 32 * s, oc + 32 * s + 32), 512)
+            gs = T["gs_%d" % h][:, c[0]:c[1]]
+            fns = [lambda gs=gs: PE.matmul(el[:, 0:512], T.idm[:], gs, True, False)]
+            fns += [(lambda j=j: PE.matmul(el[:, 64 * j:64 * j + 64], T.idn[:], x, False, j == 7)) for j in range(8)]
+            add("P", "c", fns, [("idm", 0, 128), ("idn", 0, 128), ("gs_%d" % h, c[0], c[1]), ("fe", c0, c0 + 64)], [d[1]], 1024 * 0.85)
+            acp(o("cs_%d" % h, *c), d, 512, AF.Relu)
+        out = o("au_%d" % h, 64, 128)
+        count(out, "cs_%d" % h)
+        st, shw, shl = (o(n + "_%d" % h, 0, 64) for n in ("st", "shw", "shl"))
+        vts(st, out, -16.0, OP.mult, 64)
+        vtt(shw, st, o("kc1", 0, 64), OP.add, 64)
+        vtt(shl, o("kc2", 0, 64), st, OP.subtract, 64)
+
+    def visit(t, a, h):
+        q = (r + a) % N
+        win = o("notes", q * SL, q * SL + H)
+        nm = lambda n: n + "_%d" % h
+        for c in SUBS:
+            w = c[1] - c[0]
+            offs = o(nm("off"), c[0] // 16, c[1] // 16)
+            if c == SUBS[0]:
+                vgtt(o(nm("cm"), *c), win, offs, o(nm("fvs"), 0, w), OP.is_lt, w)
+                continue
+            agather(o(nm("gx"), *c), win, offs, w)
+            vtt(o(nm("cm"), *c), o(nm("gx"), *c), o(nm("fvx"), 0, w), OP.is_lt, w)
+        s64 = lambda n: o(nm(n), 0, 64)
+        acp(s64("sq"), s64("cc"), 64, AF.Square, bias=T.con[:, 0:1])
+        acp(s64("rr"), s64("cc"), 64, AF.Identity, bias=T.con[:, 1:2])
+        vts(s64("vs"), s64("sq"), 1.0 / 32, OP.mult, 64, -13.0 / 32, OP.add)
+        count(o(nm("nn"), 0, 64), nm("cm"))
+        kap = T["kap%d" % t][:, q:q + 1] if t else -8.0
+        vts(o(nm("nn"), 64, 128), o(nm("nn"), 0, 64), float(W), OP.mult, 64, kap, OP.add, sreg=("kap%d" % t, q, q + 1) if t else None)
+        vtt(o(nm("nn"), 128, 192), o(nm("nn"), 64, 128), s64("vs"), OP.add, 64)
+        vtt(s64("qi"), o(nm("nn"), 128, 192), s64("rr"), OP.max, 64)
+        vts(s64("ci"), s64("qi"), 4095, OP.bitwise_and, 64)
+        if a < N - 1:
+            vcp(s64("off"), s64("ci"), 64)
+            vcp(s64("cc"), s64("ci"), 64)
+        else:
+            vts(o(nm("ci"), 64, 128), s64("qi"), 4095, OP.bitwise_and, 64)
+
+    def elect(h):
+        nm = lambda n: n + "_%d" % h
+        el = nm("el")
+        vcp(o(el, 0, 128), o(nm("ci"), 0, 128), 128)
+        ee = T[nm("ee")]
+        for s in range(1, 9):
+            w = 64 + 4 * s if s < 8 else 64
+            x = (lambda s=s, w=w: V.tensor_tensor(ee[:, s - 1, 0:w], T[nm("ci")][:, 4 * s - (w - 64):4 * s - (w - 64) + w], T[el][:, 128 - w:128], OP.is_equal))
+            add("V", "c", [x], [(nm("ci"), 0, 128), (el, 0, 128)], [(nm("ee"), 96 * s - 96, 96 * s)], w * CY)
+        first = [True]
+        for s in range(1, 9):
+            cols = [0, 4 * s] if s < 8 else [0]
+            for c in cols:
+                st, sp = first[0], s == 8
+                first[0] = False
+                add("P", "c", [lambda s=s, c=c, st=st, sp=sp: PE.matmul(T[nm("nn")][:, 192:256], T.idb[:], ee[:, s - 1, c:c + 64], st, sp)],
+                    [("idb", 0, 128), (nm("ee"), 96 * s - 96, 96 * s)], [(el + "m", 0, 64)], 64 * 0.85)
+        lastm = len(ops) - 1
+        banks[nm("nn")]["P"] = lastm
+        hist[nm("nn")] = hist.get(nm("nn"), []) + [(lastm, 192, 256, True)]
+        kk = T[nm("kk")]
+        K = lambda w: (kk[:, w, :], (nm("kk"), 64 * w, 64 * w + 64))
+        m = o(nm("nn"), 192, 256)
+        vtt(K(0), m, o(nm("shw"), 0, 64), OP.add, 64)
+        vtt(K(1), o(nm("shl"), 0, 64), m, OP.subtract, 64)
+
+        def tree(src, op, dst):
+            w = 64
+            for t in ("t1", "t2", "t3"):
+                w //= 2
+                x, y = T[src], T[nm(t)]
+                vtt((y[:], (nm(t), 0, 99)), (x[:, :, 0:w], (src, 0, 128)), (x[:, :, w:2 * w], (src, 0, 128)), op, 2 * w)
+                src = nm(t)
+            dst(T[src])
+        mx = nm("mx")
+
+        def top(x):
+            for w in range(2):
+                vtt(o(mx, 8 * w, 8 * w + 4), (x[:, w, 0:4], (nm("t3"), 0, 99)), (x[:, w, 4:8], (nm("t3"), 0, 99)), OP.max, 4)
+        tree(nm("kk"), OP.max, top)
+        for w in range(2):
+            oh = (T[nm("oh")][:, w, :], (nm("oh"), 64 * w, 64 * w + 64))
+            vgtt(oh, o(mx, 8 * w, 8 * w + 4), o("offx", 0, 4), K(w), OP.is_equal, 64)
+            vtt((T[nm("pp")][:, w, :], (nm("pp"), 64 * w, 64 * w + 64)), oh, o(el, 64, 128), OP.mult, 64)
+
+        def fin(x):
+            vtt((T.val[:, :, 4 * h:4 * h + 4], ("val", 8 * h, 8 * h + 8)), (x[:, :, 0:4], (nm("t3"), 0, 99)), (x[:, :, 4:8], (nm("t3"), 0, 99)), OP.add, 8)
+        tree(nm("pp"), OP.add, fin)
+
+    VALR = ("val", 0, 16)
+
+    def split(w):
+        v = (T.val[:, w, :], VALR)
+        vts(o("hl", 16 * w, 16 * w + 8), v, 4032, OP.bitwise_and, 8)
+        vts(o("hl", 16 * w + 8, 16 * w + 16), v, 63, OP.bitwise_and, 8)
+        vgtt(o("xx", 256 * w, 256 * w + 256), o("hl", 16 * w, 16 * w + 16), o("offq", 0, 16), o("dm", 0, 256), OP.mult, 256)
+
+    def rep(out, w, l0, l1):
+        mms(out, [(l0, o("xx", 256 * w, 256 * w + 128)), (l1, o("xx", 256 * w + 128, 256 * w + 256))], 128)
+
+    BLK = o("blk", 0, 128)
+
+    def won(t):
+        split(0)
+        if t < ROUNDS - 1:
+            rep(o("el_1", 192, 320), 0, cnt(0), cnt(1))
+            acp(o("hw", P0 + 128 * t, P0 + 128 * t + 128), o("el_1", 192, 320), 128)
+
+    def book(t):
+        rep(o("au_0", 128, 256), 0, BLK, BLK)
+        acp(o("yhs", 128 * t, 128 * t + 128), o("au_0", 128, 256), 128)
+        dma("S", "yh%d" % t, T.yh[:, 128 * t:128 * t + 128], T.yhs[0:128:16, 128 * t:128 * t + 128], [("yhs", 128 * t, 128 * t + 128)], [("yh", 128 * t, 128 * t + 128)])
+        if t == ROUNDS - 1:
+            return
+        vcp(o("hlb", 0, 16), o("hl", 0, 16), 16)
+        mms(o("au_1", 128, 144), [(o("ones", 0, 128), o("hlb", 0, 16))], 16)
+        ks, ki, kj = o("ks", 0, 1), o("ki", 0, 1), o("kj", 0, 1)
+        add("V", "c", [lambda: V.tensor_reduce(T.ks[:, 0:1], T.au_1[:, 128:144], AxisListType.X, OP.add)], [("au_1", 128, 144)], [("ks", 0, 1)], 64.0)
+        vcp(ki, ks, 1)
+        vts(kj, ki, 255, OP.bitwise_and, 1)
+        vts(o("kap%d" % (t + 1), r, r + 1), kj, -8.0, OP.add, 1)
+        vcp(o("msg%d" % t, 136, 137), kj, 1)
+
+    def lost(t):
+        lval = (T.val[:, 1, :], VALR)
+        vcp(o("loff", 0, 8), lval, 8)
+        split(1)
+        vcp(o("lv", 0, 8), lval, 8)
+        rep(o("el_0", 192, 320), 1, BLK, BLK)
+        xo, xc, xn = (o(n, 0, 128) for n in ("xo", "xc", "xn"))
+        fv = o("fe", P0 + 128 * t, P0 + 128 * t + 128)
+        own = r * SL
+        agather(xo, o("notes", own, own + H), o("loff", 0, 8), 128)
+        pd, px = o("nn_0", 256, 384), o("nn_1", 256, 384)
+        mms(pd, [(o("idn", 0, 128), fv), (o("idm", 0, 128), xo)], 128)
+        for b in range(8):
+            w = 16 * b + 16
+            vts((T.eq[:, b, 128 - w:128], ("eq", 128 * b, 128 * b + 128)), (T.el_0[:, 192:192 + w], ("el_0", 192, 320)), T.lv[:, b:b + 1], OP.is_equal, w, sreg=("lv", 0, 8))
+        dg = (T.eq[:, :, 112:128], ("eq", 0, 1024))
+        vtt(dg, dg, (T.dt[:], ("dt", 0, 128)), OP.mult, 128)
+        for b in range(8):
+            w = 16 * b + 16
+            add("V", "c", [lambda b=b, w=w: V.tensor_reduce(T.dd[:, b:b + 1], T.eq[:, b, 128 - w:128], AxisListType.X, OP.max)], [("eq", 128 * b, 128 * b + 128)], [("dd", b, b + 1)], max(64, w) * CY)
+        vts(xc, pd, 32.0, OP.min, 128, -32.0, OP.max)
+        mms(px, [(o("idn", 0, 128), xo), (o("idn", 0, 128), xc)], 128)
+        acp(xn, px, 128)
+        vtt(o("d1", 0, 8), o("dd", 0, 8), o("md", 0, 8), OP.mult, 8)
+        vtt(o("d2", 0, 8), o("d1", 0, 8), o("lv", 0, 8), OP.max, 8)
+        oo = o("msg%d" % t, 0, 8) if t < ROUNDS - 1 else o("loff", 0, 8)
+        vcp(oo, o("d2", 0, 8), 8)
+        add("V", "c", [lambda: V.tensor_copy(T.notes[:, own:own + SL].indirect(oo[0]), xn[0])], [xn[1], oo[1]], [("notes", own, own + SL)], 50 + 128 * 3.0)
+        if t < ROUNDS - 1:
+            vcp(o("msg%d" % t, 8, 136), xn, 128)
+
+    def send(t):
+        m = "msg%d" % t
+        fill(m, 137, MS, 0)
+        others = [T.cores[(r - a) % N] for a in range(1, N)]
+        mask = topo.mask(core, others[0])
+
+        def fn():
+            ids = [DstId(rid=topo.addr(c)[0], pnc=topo.addr(c)[1]) for c in others]
+            dst = T["inb%d" % t][:, r * MS:r * MS + MS]
+            return g.remote_dma_fused([RemoteDMATransfer(dst_ids=ids, dma_engine_mask=mask, remote_sem=T.sem["m%d_%d" % (t, r)],
+                                                         srcs=[T[m][:]], dsts=[dst for c in ids], alu_op=0)], local_sem=T.sem.msem)
+        ne = len(topo.engines(core, others[0]))
+        s = add("G", "r", [fn], [(m, 0, MS)], [], 1000.0, name=("msem", ne))
+        for a in range(1, N):
+            q = (r + a) % N
+            add("X", "a", [], [], [("inb%d" % t, q * MS, q * MS + MS)], 2500.0, ("m%d_%d" % (t, q), ne), extra=[s])
+
+    def take(t, a):
+        q = (r + a) % N
+        inb = "inb%d" % t
+        x = T[inb]
+        add("V", "c", [lambda: V.tensor_copy(T.notes[:, q * SL:q * SL + SL].indirect(x[:, q * MS:q * MS + 8]), x[:, q * MS + 8:q * MS + 136])],
+            [(inb, q * MS, q * MS + MS)], [("notes", q * SL, q * SL + SL)], 50 + 128 * 3.0)
+        vts(o("kap%d" % (t + 1), q, q + 1), o(inb, q * MS + 136, q * MS + 137), -8.0, OP.add, 1)
+
+    for t in range(ROUNDS):
+        for h in range(2):
+            heads(t, h)
+        for h in range(2):
+            fvx(t, h)
+        for a in range(N):
+            if t and a:
+                take(t - 1, a)
+            for h in range(2):
+                visit(t, a, h)
+            if t == 0 and a == 0:
+                tables()
+            if a in (SHARE_AT, SHARE_AT + 1):
+                shares(t, a - SHARE_AT)
+            if a == 2 and t < ROUNDS - 1:
+                convert(t + 1)
+        for h in range(2):
+            elect(h)
+        if t < ROUNDS - 1:
+            won(t)
+            lost(t)
+            book(t)
+            send(t)
+        else:
+            lost(t)
+            won(t)
+            book(t)
+    dma("S", "yl", T.yl[:], T.notes[:, r * SL:r * SL + H], [("notes", r * SL, r * SL + H)], [("yl", 0, 1)], 5000.0)
+    return ops
+
+
+def order(ops):
+    n = len(ops)
+    succ = [[] for _ in range(n)]
+    for i, x in enumerate(ops):
+        for u in x["d"]:
+            succ[u].append(i)
+    missing = [len(x["d"]) for x in ops]
+    avail = [0.0] * n
+    ready = {}
+    for i in range(n):
+        if not missing[i]:
+            ready.setdefault(ops[i]["e"], []).append(i)
+    free = {}
+    seq = []
+    start = [0.0] * n
+    while len(seq) < n:
+        best = None
+        for e, lst in ready.items():
+            if not lst:
+                continue
+            f = 0.0 if e == "X" else free.get(e, 0.0)
+            t0 = min(max(f, avail[i]) for i in lst)
+            i = min(j for j in lst if max(f, avail[j]) <= t0 + 1e-6)
+            if best is None or t0 < best[0]:
+                best = (t0, i, e)
+        t0, i, e = best
+        ready[e].remove(i)
+        x = ops[i]
+        end = t0 + x["t"]
+        start[i] = t0
+        free[e] = t0 + (60.0 if x["k"] == "d" else x["t"])
+        seq.append(i)
+        for j in succ[i]:
+            avail[j] = max(avail[j], end + HOP)
+            missing[j] -= 1
+            if not missing[j]:
+                ready.setdefault(ops[j]["e"], []).append(j)
+    return seq, start
+
+
+def rank_program(g, core, T, topo):
+    r = T.rank_of(core)
+    if r is None:
+        return
+    ops = build(g, r, T, topo)
+    seq, _ = order(ops)
+    queue = {"V": g.vector, "A": g.scalar, "P": g.tensor, "G": g, "S": g.sync}
+    total = {}
+    key = {}
+    clock = {}
+    known = {e: {} for e in queue}
+    for i in seq:
+        x = ops[i]
+        e = x["e"]
+        if x["k"] == "a":
+            key[i] = x["n"]
+            clock[i] = {x["n"][0]: x["n"][1]}
+            total[x["n"][0]] = x["n"][1]
+            continue
+        kn = known[e]
+        need = {}
+        for u, raw in x["d"].items():
+            if ops[u]["e"] == e and ops[u]["k"] == "c" and x["k"] == "c" and not raw:
+                continue
+            s, c = key[u]
+            if kn.get(s, 0) < c:
+                need.setdefault(s, []).append((c, u))
+        for s in sorted(need, key=lambda z: -max(need[z])[1]):
+            c, u = max(need[s])
+            if kn.get(s, 0) < c:
+                queue[e].wait_ge(T.sem[s], c)
+                for a, b in clock[u].items():
+                    kn[a] = max(kn.get(a, 0), b)
+        if x["k"] == "c":
+            s = "p" + e
+            for f in x["f"]:
+                f().then_inc(T.sem[s], 1)
+                total[s] = total.get(s, 0) + 1
+            key[i] = (s, total[s])
+        elif x["k"] == "d":
+            s = "d_" + x["n"]
+            x["f"][0]().then_inc(T.sem[s], 16)
+            total[s] = 16
+            key[i] = (s, 16)
+        else:
+            x["f"][0]()
+            s, c = x["n"]
+            total[s] = total.get(s, 0) + c
+            key[i] = (s, total[s])
+        clock[i] = dict(kn)
+        clock[i][key[i][0]] = key[i][1]
+    for s in sorted(total):
+        if known["G"].get(s, 0) < total[s]:
+            g.wait_ge(T.sem[s], total[s])

@@ -3,51 +3,59 @@ from concourse.mybir import AluOpType as OP, AxisListType, ActivationFunctionTyp
 
 N = 8
 H, P0, B, ROUNDS = 4096, 1536, 128, 4
-SL = H + B
+SL = B + H
 W = 613 + 4096 * 129
 R = (9 * W // 4096) * 4096
-SUBS = ((576, 1024), (0, 256), (256, 448), (448, 576))
-SHARE_AT = 4
+M23 = 2.0 ** 23
+KAP0 = -8.0 - R - M23
+BIG = 2.0 ** 18
 MS = 144
+E = 136
+ROW = [("fp_0", 8 * b * (b + 1), 8 * (b + 1) * (b + 2)) if b < 6 else ("fp_1", 112 * (b - 6), 112 * (b - 6) + 16 * b + 16) for b in range(8)]
 
-SCRATCH = {
-    "notes": ("sbuf", [128, N * SL], "bfloat16"),
-    "yy": ("sbuf", [128, 16, 128], "float16"),
-    "cf": ("sbuf", [128, 512], "float16"),
-    "dt": ("sbuf", [128, 8, 16], "bfloat16"),
-    "eq": ("sbuf", [128, 8, 128], "bfloat16"),
-    "val": ("sbuf", [128, 2, 8], "int32"),
-}
-for _d, _l in (("bfloat16", (("fe", 2048), ("hw", 2048), ("cnt", 2048), ("hdb", 192), ("dm", 256), ("blk", 128), ("vv", 128), ("vt", 128), ("idn", 128),
-                             ("idm", 128), ("idb", 128), ("ones", 128), ("xo", 128), ("xc", 128), ("hlb", 16), ("xx", 512))),
-               ("int32", (("ci0", 512), ("hdi", 96), ("hdx", 192), ("ia", 128), ("ib", 128), ("ja", 128), ("jb", 128), ("ka", 128), ("kb", 128), ("iq", 32),
-                          ("ix", 4), ("imd", 8), ("hl", 32), ("d2", 8), ("ki", 1), ("kj", 1))),
-               ("uint16", (("offq", 32), ("offx", 4), ("loff", 8), ("offc", 128 * ROUNDS))),
-               ("float32", (("md", 8), ("kc1", 64), ("kc2", 64), ("lv", 8), ("dd", 8), ("d1", 8), ("xn", 128), ("con", 2), ("ks", 1), ("yhs", 512)))):
+CV = (20, 8, 8, 8)
+AORD = ("ga", "sq", "vs", "sg", "vk")
+SH = ("AA", "AA", "AA", "AA")
+SLACK = (100.0, 300.0)
+EARLY = 4000.0
+TP = 2
+AHEAD = 1500.0
+HV = (32, 16)
+WN = "A"
+SP = 256
+
+SCRATCH = {"notes": ("sbuf", [128, N * SL], "bfloat16")}
+for _d, _l in (("bfloat16", (("fe", 2048), ("hw", 2048), ("cnt", 2048), ("F0", 2048), ("F1", 2048), ("cs", 2048), ("gs", 1024), ("hdb", 192),
+                             ("dm", 128), ("dmp", 128), ("blk", 128), ("nblk", 8), ("vv", 128), ("vt", 128), ("idn", 128), ("idm", 128), ("idb", 128),
+                             ("ones", 128), ("xo", 128), ("xc", 128), ("hl", 128), ("rv", 128), ("rot", 1024), ("ee", 1024), ("xb", 1024),
+                             ("jc", E), ("gcol", E), ("ofb", E), ("za", E), ("zb", E), ("zm", E), ("zr", E), ("rs", 8 * E), ("dp", E), ("dn", E),
+                             ("d0", 2 * E), ("nr", 2 * E), ("zer", E), ("pen", 16), ("c21", 8), ("ct", 576))),
+               ("float16", (("c16", 128), ("xy", 256))),
+               ("int32", (("ci0", 512), ("hdi", 96), ("hdx", 192), ("ia", 128), ("ib", 128), ("ja", 128), ("jb", 128), ("ka", 128), ("kb", 128),
+                          ("iu", 128), ("iz", E), ("ix", 8), ("ki", 1), ("kj", 1))),
+               ("uint16", (("offx", 8), ("loff", 8), ("offc", 128 * ROUNDS))),
+               ("float32", (("col", 8), ("con", 8), ("run", 2 * E), ("er", 2 * E), ("dd", 8), ("d1", 8), ("ks", 1), ("kw", 128), ("yhs", 512),
+                            ("kown", 8)))):
     for _n, _w in _l:
         SCRATCH[_n] = ("sbuf", [128, _w], _d)
 for _h in range(2):
-    for _n, _w, _d in (("gx", 1024, "bfloat16"), ("cm", 1024, "bfloat16"), ("gs", 1024, "bfloat16"), ("cs", 1024, "bfloat16"), ("fvs", 512, "bfloat16"),
-                       ("off", 64, "uint16"), ("ci", 128, "int32"), ("cc", 64, "float32"), ("sq", 64, "float32"), ("vs", 64, "int32"),
-                       ("rr", 64, "float32"), ("qi", 64, "int32"), ("st", 64, "float32"), ("shw", 64, "float32"),
-                       ("shl", 64, "float32"), ("mx", 16, "float32")):
+    for _n, _w, _d in (("gx", 1024, "bfloat16"), ("cm", 1024, "bfloat16"), ("off", 64, "uint16"), ("ci", 64, "int32"), ("cc", 64, "float32"),
+                       ("sq", 64, "float32"), ("vs", 64, "float32"), ("qi", 64, "int32")):
         SCRATCH[_n + "_%d" % _h] = ("sbuf", [128, _w], _d)
-    SCRATCH["ee_%d" % _h] = ("sbuf", [128, 8, 96], "bfloat16")
-    for _n, _w in (("kk", 64), ("t1", 32), ("t2", 16), ("t3", 8), ("oh", 64), ("pp", 64)):
-        SCRATCH[_n + "_%d" % _h] = ("sbuf", [128, 2, _w], "float32")
-    for _n in ("fvx", "nn", "el", "au"):
+    SCRATCH["vk_%d" % _h] = ("sbuf", [128, 128], "float32")
+    for _n in ("nn", "df", "fp"):
         SCRATCH[_n + "_%d" % _h] = ("psum", [128, 512], "float32")
-for _t in range(ROUNDS - 1):
-    SCRATCH["msg%d" % _t] = ("sbuf", [128, MS], "uint16")
+for _n in ("sh", "key"):
+    SCRATCH[_n] = ("psum", [128, 512], "float32")
+for _t in range(ROUNDS):
     SCRATCH["inb%d" % _t] = ("sbuf", [128, N * MS], "uint16")
-    SCRATCH["kap%d" % (_t + 1)] = ("sbuf", [128, N], "float32")
+    SCRATCH["kap%d" % _t] = ("sbuf", [128, N], "float32")
 
 DMAS = ["comp0", "comp1", "hd", "fe0", "fe1", "lim", "hwa", "hwb", "yh0", "yh1", "yh2", "yh3", "yl"]
 SEMAPHORES = (["pV", "pA", "pP", "pG", "lsem", "msem"] + ["d_" + n for n in DMAS] + ["lim%d" % q for q in range(N)]
               + ["m%d_%d" % (t, q) for t in range(ROUNDS - 1) for q in range(N)])
 
-CY = 1.0
-HOP = 80.0
+TIMES = {"cy": 1.0, "pe": 0.5, "hop": 215.0, "gather": 1.5, "scatter": 3.5, "note": 4000.0}
 
 
 def build(g, r, T, topo):
@@ -56,6 +64,8 @@ def build(g, r, T, topo):
     banks = {}
     core = T.cores[r]
     V, A, PE, S = g.vector, g.scalar, g.tensor, g.sync
+    CY, PC, GA, SC = (TIMES[n] for n in ("cy", "pe", "gather", "scatter"))
+    late = [False, 0.0]
 
     def add(eng, kind, fns, reads, writes, dur, name=None, extra=()):
         i = len(ops)
@@ -69,13 +79,15 @@ def build(g, r, T, topo):
         for buf, lo, hi in writes:
             for acc in hist.get(buf, ()):
                 if acc[1] < hi and lo < acc[2]:
-                    deps.setdefault(acc[0], False)
+                    deps[acc[0]] = deps.get(acc[0], False) or eng != "P" or ops[acc[0]]["e"] != "P"
         for buf in sorted({x[0] for x in list(reads) + list(writes)}):
             if SCRATCH.get(buf, ("",))[0] == "psum":
                 last = banks.setdefault(buf, {})
                 for e, u in last.items():
                     if e != eng:
                         deps[u] = True
+                    else:
+                        deps.setdefault(u, False)
                 last[eng] = i
         for buf, lo, hi in writes:
             h = [a for a in hist.get(buf, []) if not (lo <= a[1] and a[2] <= hi)]
@@ -84,45 +96,63 @@ def build(g, r, T, topo):
         for buf, lo, hi in reads:
             hist.setdefault(buf, []).append((i, lo, hi, False))
         deps.pop(i, None)
-        ops.append({"e": eng, "k": kind, "f": fns, "d": deps, "t": dur, "n": name})
+        ops.append({"e": eng, "k": kind, "f": fns, "d": deps, "t": dur, "n": name, "late": late[0], "u": late[1]})
         return i
 
-    def o(name, lo, hi):
-        return (T[name][:, lo:hi], (name, lo, hi))
+    def o(name, lo, hi, step=1):
+        return (T[name][:, lo:hi:step] if step > 1 else T[name][:, lo:hi], (name, lo, hi))
 
-    def cyc(n, *ops2):
-        both = all(SCRATCH.get(x[1][0], ("",))[0] == "sbuf" for x in ops2)
-        return max(64, n * (2 if both and len(ops2) == 2 else 1)) * CY
+    def narrow(*xs):
+        return 0.5 if all(SCRATCH[x[1][0]][2] in ("bfloat16", "float16", "uint16") for x in xs) else 1.0
 
     def vtt(out, a, b, op, n):
-        return add("V", "c", [lambda: V.tensor_tensor(out[0], a[0], b[0], op)], [a[1], b[1]], [out[1]], cyc(n, a, b))
+        both = all(SCRATCH[x[1][0]][0] == "sbuf" for x in (a, b))
+        return add("V", "c", [lambda: V.tensor_tensor(out[0], a[0], b[0], op)], [a[1], b[1]], [out[1]], max(64, n * (2 if both else 1)) * CY)
 
-    def vts(out, a, s1, op, n, s2=None, op1=None, sreg=None, half=False):
+    def vts(out, a, s1, op, n, s2=None, op1=None):
+        col = isinstance(s1, tuple)
+        x = s1[0] if col else s1
+
         def f():
             if op1 is None:
-                return V.tensor_scalar(out[0], a[0], s1, None, op)
-            return V.tensor_scalar(out[0], a[0], s1, s2, op, op1)
-        return add("V", "c", [f], [a[1]] + ([sreg] if sreg else []), [out[1]], max(64, n * (0.5 if half else 1)) * CY)
+                return V.tensor_scalar(out[0], a[0], x, None, op)
+            return V.tensor_scalar(out[0], a[0], x, s2, op, op1)
+        return add("V", "c", [f], [a[1]] + ([s1[1]] if col else []), [out[1]], max(64, n * narrow(out, a)) * CY)
 
     def vcp(out, a, n):
-        return add("V", "c", [lambda: V.tensor_copy(out[0], a[0])], [a[1]], [out[1]], max(64, n) * CY)
+        return add("V", "c", [lambda: V.tensor_copy(out[0], a[0])], [a[1]], [out[1]], max(64, n * narrow(out, a)) * CY)
 
-    def fill(name, lo, hi, x, dur=64.0):
-        return add("V", "c", [lambda: V.memset(T[name][:, lo:hi], x)], [], [(name, lo, hi)], dur)
+    def scan(out, a, b, op0, op1, n):
+        return add("V", "c", [lambda: V.tensor_tensor_scan(out[0], a[0], b[0], 0.0, op0, op1)], [a[1], b[1]], [out[1]], max(64, n) * CY)
 
-    def acp(out, a, n, func=AF.Copy, **kw):
-        return add("A", "c", [lambda: A.activation(out[0], a[0], func, **kw)], [a[1]] + ([("con", 0, 2)] if kw else []), [out[1]], 65 + n * CY)
+    def fill(x, v, n=64):
+        return add("V", "c", [lambda: V.memset(x[0], v)], [], [x[1]], max(64, n * narrow(x)) * CY)
+
+    def act(out, a, n, func=AF.Copy, bias=None, scale=None, acc=None):
+        kw = {}
+        if bias:
+            kw["bias"] = bias[0]
+        if scale:
+            kw["scale"] = scale
+        if acc:
+            kw["accum_out"] = acc[0]
+        return add("A", "c", [lambda: A.activation(out[0], a[0], func, **kw)], [a[1]] + ([bias[1]] if bias else []),
+                   [out[1]] + ([acc[1]] if acc else []), 65 + n * CY)
 
     def agather(out, win, offs, n):
-        return add("A", "c", [lambda: A.activation(out[0], win[0].indirect(offs[0]), AF.Copy)], [win[1], offs[1]], [out[1]], 65 + n * 1.5 * CY)
+        return add("A", "c", [lambda: A.activation(out[0], win[0].indirect(offs[0]), AF.Copy)], [win[1], offs[1]], [out[1]], 65 + n * GA * CY)
+
+    def vgather(out, win, offs, n):
+        return add("V", "c", [lambda: V.tensor_copy(out[0], win[0].indirect(offs[0]))], [win[1], offs[1]], [out[1]], 50 + n * GA * CY)
 
     def vgtt(out, win, offs, b, op, n):
-        return add("V", "c", [lambda: V.tensor_tensor(out[0], win[0].indirect(offs[0]), b[0], op)], [win[1], offs[1], b[1]], [out[1]], 50 + n * 1.5 * CY)
+        return add("V", "c", [lambda: V.tensor_tensor(out[0], win[0].indirect(offs[0]), b[0], op)], [win[1], offs[1], b[1]], [out[1]], 50 + n * GA * CY)
 
-    def mms(out, pairs, n):
-        last = len(pairs) - 1
-        fns = [(lambda l=l, x=x, i=i: PE.matmul(out[0], l[0], x[0], i == 0, i == last)) for i, (l, x) in enumerate(pairs)]
-        return add("P", "c", fns, sorted({x[1] for p in pairs for x in p}), [out[1]], len(pairs) * max(64, n) * 0.85 * CY)
+    def mm(steps, first=True, last=True, again=False):
+        k = len(steps) - 1
+        fns = [(lambda s=s, i=i: PE.matmul(s[0][0], s[1][0], s[2][0], first and i == 0, last and i == k)) for i, s in enumerate(steps)]
+        outs = sorted({s[0][1] for s in steps})
+        return add("P", "c", fns, sorted({x[1] for s in steps for x in s[1:3]}), outs, sum(max(64, s[3]) for s in steps) * PC * CY)
 
     def dma(q, name, out, in_, reads, writes, dur=2500.0):
         eng = {"S": S, "A": A}[q]
@@ -132,42 +162,39 @@ def build(g, r, T, topo):
         return o("cnt", 128 * a, 128 * a + 128)
 
     def count(out, buf):
-        x = T[buf]
-        return mms(out, [(cnt(a), (x[:, a:1024:16], (buf, 0, 1024))) for a in range(16)], 64)
+        return mm([(out, cnt(a), (T[buf][:, a:1024:16], (buf, 0, 1024)), 64) for a in range(16)])
 
-    dma("A", "lim", T.notes[:, r * SL:r * SL + H], T.lim[:], [], [("notes", r * SL, r * SL + H)], 5000.0)
-    dma("S", "comp0", T.ci0[:, 0:128], T.comp[:, 0:128], [], [("ci0", 0, 128)])
+    w128 = lambda n: o(n, 0, 128)
+    IDN, IDM, IDB, BLK = w128("idn"), w128("idm"), w128("idb"), w128("blk")
+    con = lambda i: o("con", i, i + 1)
+    note = lambda q: o("notes", q * SL + B, q * SL + SL)
+    slot = lambda q: o("notes", q * SL, q * SL + SL)
+    goods = lambda t: o("fe", P0 + 128 * t, P0 + 128 * t + 128)
+
+    dma("A", "lim", note(r)[0], T.lim[:], [], [note(r)[1]], 5500.0)
     dma("S", "hd", T.hdi[:], T.hd[:], [], [("hdi", 0, 96)])
-    dma("S", "fe1", T.fe[:, P0:2048], T.feat[:, P0:2048], [], [("fe", P0, 2048)])
-    dma("S", "fe0", T.fe[:, 0:P0], T.feat[:, 0:P0], [], [("fe", 0, P0)], 4000.0)
-    dma("S", "comp1", T.ci0[:, 128:512], T.comp[:, 128:512], [], [("ci0", 128, 512)])
+    dma("S", "comp0", T.ci0[:, 0:128], T.comp[:, 0:128], [], [("ci0", 0, 128)])
+    dma("S", "fe1", T.fe[:, P0:2048], T.feat[:, P0:2048], [], [("fe", P0, 2048)], 3000.0)
+    dma("S", "fe0", T.fe[:, 0:P0], T.feat[:, 0:P0], [], [("fe", 0, P0)], 5000.0)
+    dma("S", "comp1", T.ci0[:, 128:512], T.comp[:, 128:512], [], [("ci0", 128, 512)], 5000.0)
 
     def iota(name, w, pat, base, ch):
         out = T[name]
         kw = {} if SCRATCH[name][2] == "int32" else {"allow_small_or_imprecise_dtypes": True}
-        add("G", "c", [lambda: g.iota(out[:, 0:w], pat, base, ch, **kw)], [], [(name, 0, w)], 130 + 2 * w)
+        add("G", "c", [lambda: g.iota(out[:, 0:w], pat, base, ch, **kw)], [], [(name, 0, w)], 130 + 2 * w * CY)
+
+    def select(out, a, pat, base, ch, n):
+        add("G", "c", [lambda: g.affine_select(out[0], a[0], pat, OP.is_ge, 0.0, base, ch)], [a[1]], [out[1]], 170 + 2 * n * CY)
     iota("ia", 128, [[0, 128]], 0, 1)
     iota("ib", 128, [[1, 128]], 0, 0)
-    iota("iq", 32, [[1, 32]], 0, 0)
-    iota("imd", 8, [[16, 8]], H, 0)
-    iota("kc1", 64, [[-1, 16], [0, 4]], 15, 0)
-    iota("kc2", 64, [[-1, 16], [0, 4]], 0, 0)
-    w128 = lambda n: o(n, 0, 128)
-    fill("con", 0, 1, 16.0)
-    fill("con", 1, 2, float(R))
-    zeros = fill("hw", 0, 2048, 0.0, 1024.0)
-    vts(w128("ja"), w128("ia"), 4, OP.arith_shift_right, 128)
-    vts(w128("jb"), w128("ib"), 4, OP.arith_shift_right, 128)
-    vts(w128("ka"), w128("ia"), 15, OP.bitwise_and, 128)
-    vts(w128("kb"), w128("ib"), 15, OP.bitwise_and, 128)
-    vtt(w128("blk"), w128("ja"), w128("jb"), OP.is_equal, 128)
-    vtt(w128("dm"), w128("ka"), w128("kb"), OP.is_equal, 128)
-    vcp(o("dm", 128, 256), w128("dm"), 64)
-    vts(w128("vt"), w128("blk"), -99.0, OP.mult, 128, 99.0, OP.add, half=True)
-    vtt(w128("vv"), w128("vt"), w128("kb"), OP.add, 128)
-    vtt(w128("idn"), w128("blk"), w128("dm"), OP.mult, 128)
-    vts(w128("idm"), w128("idn"), -1.0, OP.mult, 128, half=True)
-
+    iota("iu", 128, [[-1, 128]], 128, 1)
+    iota("iz", E, [[0, 8], [1, 17]], 1, 1)
+    iota("jc", E, [[0, 8], [1, 17]], 0, 0)
+    iota("gcol", E, [[1, 8], [0, 17]], 0, 0)
+    iota("ix", 8, [[17, 8]], E + 16, 0)
+    zeros = fill(o("hw", 0, 2048), 0.0, 2048)
+    for i, v in enumerate((16.0, M23 - 0.5, -100.0, KAP0)):
+        fill(con(i), v)
     vts(o("hdx", 0, 96), o("hdi", 0, 96), 4032, OP.bitwise_and, 96)
     vts(o("hdx", 96, 192), o("hdi", 0, 96), 63, OP.bitwise_and, 96)
     vcp(o("hdb", 0, 192), o("hdx", 0, 192), 192)
@@ -177,232 +204,264 @@ def build(g, r, T, topo):
     i2 = dma("S", "hwb", T.hw[1:128:16, 0:P0], T.hdb[:, 96:192], [("hdb", 96, 192)], [("hw", 0, P0)])
     ops[i2]["d"][zeros] = True
     hist["hw"] = keep + [(i2, 0, P0, True)]
+    vts(w128("ja"), w128("ia"), 4, OP.arith_shift_right, 128)
+    vts(w128("jb"), w128("ib"), 4, OP.arith_shift_right, 128)
+    vts(w128("ka"), w128("ia"), 15, OP.bitwise_and, 128)
+    vts(w128("kb"), w128("ib"), 15, OP.bitwise_and, 128)
+    vtt(BLK, w128("ja"), w128("jb"), OP.is_equal, 128)
+    vts(w128("vt"), BLK, -99.0, OP.mult, 128, 99.0, OP.add)
+    vtt(w128("vv"), w128("vt"), w128("kb"), OP.add, 128)
     for a in range(16):
-        vts(cnt(a), w128("vv"), float(a), OP.is_equal, 128, half=True)
+        vts(cnt(a), w128("vv"), float(a), OP.is_equal, 128)
+    vtt(IDN, w128("ia"), w128("ib"), OP.is_equal, 128)
+    vts(IDM, IDN, -1.0, OP.mult, 128)
+    vcp(o("offc", 0, 128), o("ci0", 0, 128), 128)
 
-    def convert(t):
-        c0 = 128 * t
-        vcp(o("cf", c0, c0 + 128), o("ci0", c0, c0 + 128), 128)
+    def spread(t):
+        name = "F%d" % (t % 2)
+        keep = [x for x in hist.get(name, [])]
+        done = []
         for k in range(16):
-            vts((T.yy[:, k, :], ("yy", 128 * k, 128 * k + 128)), o("cf", c0, c0 + 128), T.dm[:, k:k + 1], OP.mult, 128, sreg=("dm", 0, 128), half=True)
-        for h in range(2):
-            out = o("au_%d" % h, 256, 320)
-            mms(out, [(cnt(a), (T.yy[:, :, 64 * h + a:64 * h + 64:16], ("yy", 0, 2048))) for a in range(16)], 64)
-            vcp(o("offc", 128 * t + 64 * h, 128 * t + 64 * h + 64), out, 64)
+            hist[name] = list(keep)
+            out = (T[name][:, k:2048:16], (name, 0, 2048))
+            if t == 0:
+                vcp(out, goods(t), 128)
+            else:
+                select(out, goods(t), [[0, 128]], 0, 0, 128)
+            done.append((len(ops) - 1, 0, 2048, True))
+        hist[name] = done
+    spread(0)
 
-    convert(0)
     for a in range(1, N):
         dst = T.cores[(r - a) % N]
 
         def fn(dst=dst):
             rid, pid = topo.addr(dst)[:2]
-            return g.remote_dma(T.notes[:, r * SL:r * SL + H], T.notes[:, r * SL:r * SL + H], T.sem["lim%d" % r], T.sem.lsem, pid, rid, topo.mask(core, dst))
-        sent = add("G", "r", [fn], [("notes", r * SL, r * SL + H)], [], 1000.0, name=("lsem", len(topo.engines(core, dst))))
+            return g.remote_dma(note(r)[0], note(r)[0], T.sem["lim%d" % r], T.sem.lsem, pid, rid, topo.mask(core, dst))
+        sent = add("G", "r", [fn], [note(r)[1]], [], 1000.0, name=("lsem", len(topo.engines(core, dst))))
         q = (r + a) % N
-        add("X", "a", [], [], [("notes", q * SL, q * SL + H)], 4000.0, ("lim%d" % q, len(topo.engines(T.cores[q], core))), extra=[sent])
+        add("X", "a", [], [], [note(q)[1]], 1000.0 + (TIMES["note"] - 1000.0) * a, ("lim%d" % q, len(topo.engines(T.cores[q], core))), extra=[sent])
 
     def tables():
-        vts(w128("idb"), w128("idn"), 65536.0, OP.mult, 128, half=True)
-        fill("ones", 0, 128, 1.0)
-        vcp(o("offq", 0, 32), o("iq", 0, 32), 32)
-        vts(o("ix", 0, 4), o("ia", 0, 4), 3, OP.bitwise_and, 4)
-        vcp(o("offx", 0, 4), o("ix", 0, 4), 4)
-        vtt(o("md", 0, 8), o("imd", 0, 8), o("ka", 0, 8), OP.add, 8)
+        e = lambda n: o(n, 0, E)
+        col = lambda i: o("col", i, i + 1)
+        vcp(o("offc", 128, 512), o("ci0", 128, 512), 384)
+        fill(e("zer"), 0.0)
+        vts(o("nblk", 0, 8), o("blk", 0, 128, 16), -1.0, OP.mult, 8)
+        vtt(w128("dm"), w128("ka"), w128("kb"), OP.is_equal, 128)
+        vcp(col(0), o("ja", 0, 1), 1)
+        vts(col(1), o("ka", 0, 1), 1.0, OP.add, 1)
+        vts(col(2), o("ia", 0, 1), 1.0 / 8192, OP.mult, 1)
+        vts(w128("dmp"), w128("dm"), col(2), OP.mult, 128)
+        vts(IDB, IDN, -8192.0, OP.mult, 128)
+        fill(w128("ones"), 1.0)
+        fill(o("c21", 0, 8), 2048.0 + B)
+        fill(w128("hl"), 0.0)
+        fill(o("hl", 2, 128, 16), 2048.0)
+        vcp(o("offx", 0, 8), o("ix", 0, 8), 8)
+        vcp(col(3), o("ka", 0, 1), 1)
+        vts(o("pen", 0, 16), o("jc", 0, 16), col(3), OP.is_ge, 16, -8192.0, OP.mult)
+        vts(w128("iu"), w128("iu"), 15, OP.bitwise_and, 128)
+        vtt(w128("rv"), w128("iu"), w128("vt"), OP.add, 128)
+        for s in range(1, 9):
+            vts(o("rot", 128 * s - 128, 128 * s), w128("rv"), float(s), OP.is_equal, 128)
+        vts(e("ofb"), e("gcol"), col(0), OP.not_equal, E, 99.0, OP.mult)
+        vts(e("za"), e("jc"), col(1), OP.add, E)
+        vtt(e("zm"), e("za"), e("ofb"), OP.add, E)
+        vts(e("dp"), e("zm"), 17.0, OP.is_equal, E)
+        vts(e("dn"), e("zm"), 16.0, OP.is_equal, E, -1.0, OP.mult)
+        vts(e("iz"), e("iz"), 15, OP.bitwise_and, E)
+        vts(e("za"), e("jc"), 16.0, OP.is_equal, E, 50.0, OP.mult)
+        vtt(e("zb"), e("za"), e("ofb"), OP.add, E)
+        vtt(e("zr"), e("zb"), e("iz"), OP.add, E)
+        for s in range(8):
+            vts(o("rs", E * s, E * s + E), e("zr"), float((16 - s) % 16), OP.is_equal, E, 4096.0, OP.mult)
+        fill(o("d0", 0, 2 * E), 0.0, 2 * E)
+        for w, sign in enumerate((1.0, -1.0)):
+            fill(o("d0", E * w, E * w + E, 17), -3 * BIG * sign)
+            fill(o("d0", E * w + 16, E * w + E, 17), BIG * sign)
+        xb = o("xb", 0, 1024)
+        iota("xb", 1024, [[0, 1024]], 8192, 0)
+        ops[-1]["d"][sent] = False
+        select(xb, xb, [[-16, 8], [0, 128]], 0, 1, 1024)
+        select(xb, xb, [[16, 8], [0, 128]], 15, -1, 1024)
+        for s in range(1, 8):
+            x = o("sh", 0, E)
+            mm([(x, IDN, o("rs", E * s, E * s + E), E), (x, IDN, o("rs", 0, E), E)])
+            act(o("rs", E * s, E * s + E), x, E)
         for b in range(8):
-            vtt((T.dt[:, b, :], ("dt", 16 * b, 16 * b + 16)), o("kb", 0, 16), o("ka", 0, 16), OP.is_lt, 16)
-
-    def fvx(t, h):
-        c0 = P0 + 128 * t + 64 * h
-        x = o("fe", c0, c0 + 64)
-        name = "fvx_%d" % h
-        fns = [(lambda j=j: PE.matmul(T[name][:, 64 * j:64 * j + 64], T.idn[:], x[0], True, True)) for j in range(8)]
-        add("P", "c", fns, [("idn", 0, 128), x[1]], [(name, 0, 512)], 8 * 64 * 0.85)
-        w = SUBS[0][1] - SUBS[0][0]
-        acp(o("fvs_%d" % h, 0, w), o(name, 0, w), w)
+            w, c = 16 * b + 16, 8 * b * (b + 1)
+            x = o("sh", 0, w)
+            mm([(x, w128("dmp"), o("xb", 128 * b, 128 * b + w), w), (o("sh", w - 16, w), IDB, o("pen", 0, 16), 16)])
+            act(o("ct", c, c + w), x, w)
 
     def heads(t, h):
         oc = 128 * t + 64 * h
-        for s in range(2):
-            agather(o("gx_%d" % h, 512 * s, 512 * s + 512), o("hw", 0, 2048), o("offc", oc + 32 * s, oc + 32 * s + 32), 512)
-        out = o("au_%d" % h, 0, 64)
-        count(out, "gx_%d" % h)
+        cv = HV[min(t, 1)]
+        gx, hw = "gx_%d" % h, o("hw", 0, 2048)
+        if cv:
+            vgather(o(gx, 0, 16 * cv), hw, o("offc", oc, oc + cv), 16 * cv)
+        agather(o(gx, 16 * cv, 1024), hw, o("offc", oc + cv, oc + 64), 1024 - 16 * cv)
+        out = o("nn_%d" % h, 0, 64)
+        count(out, gx)
         vcp(o("off_%d" % h, 0, 64), out, 64)
-        acp(o("cc_%d" % h, 0, 64), out, 64)
+        act(o("cc_%d" % h, 0, 64), out, 64)
 
-    def shares(t, h):
-        oc = 128 * t + 64 * h
-        c0 = P0 + 128 * t + 64 * h
-        x, el, d = T.fe[:, c0:c0 + 64], T["el_%d" % h], o("el_%d" % h, 0, 512)
-        for s in range(2):
-            c = (512 * s, 512 * s + 512)
-            agather(o("gs_%d" % h, *c), o("fe", 0, 2048), o("offc", oc + 32 * s, oc + 32 * s + 32), 512)
-            gs = T["gs_%d" % h][:, c[0]:c[1]]
-            fns = [lambda gs=gs: PE.matmul(el[:, 0:512], T.idm[:], gs, True, False)]
-            fns += [(lambda j=j: PE.matmul(el[:, 64 * j:64 * j + 64], T.idn[:], x, False, j == 7)) for j in range(8)]
-            add("P", "c", fns, [("idm", 0, 128), ("idn", 0, 128), ("gs_%d" % h, c[0], c[1]), ("fe", c0, c0 + 64)], [d[1]], 1024 * 0.85)
-            acp(o("cs_%d" % h, *c), d, 512, AF.Relu)
-        out = o("au_%d" % h, 64, 128)
-        count(out, "cs_%d" % h)
-        st, shw, shl = (o(n + "_%d" % h, 0, 64) for n in ("st", "shw", "shl"))
-        vts(st, out, -16.0, OP.mult, 64)
-        vtt(shw, st, o("kc1", 0, 64), OP.add, 64)
-        vtt(shl, o("kc2", 0, 64), st, OP.subtract, 64)
+    def shares(t, part, parts):
+        n = 2048 // SP
+        F = "F%d" % (t % 2)
+        for s in range(n * part // parts, n * (part + 1) // parts):
+            c = SP * s
+            gs, d = o("gs", c % 1024, c % 1024 + SP), o("sh", c % 512, c % 512 + SP)
+            offs = o("offc", 128 * t + c // 16, 128 * t + (c + SP) // 16)
+            if SH[t][c // 1024] == "V":
+                vgtt(o("cs", c, c + SP), o("fe", 0, 2048), offs, o(F, c, c + SP), OP.min, SP)
+                continue
+            agather(gs, o("fe", 0, 2048), offs, SP)
+            mm([(d, IDN, o(F, c, c + SP), SP), (d, IDM, gs, SP)])
+            act(o("cs", c, c + SP), d, SP, AF.Relu)
+
+    def keys(t):
+        sign = {"V": o("blk", 0, 128, 16), "A": o("nblk", 0, 8)}
+        mm([(o("key", 0, E), IDN, o("zer", 0, E), E)], last=False)
+        for lo, hi in ((0, 128),) if SH[t][0] == SH[t][1] else ((0, 64), (64, 128)):
+            for k0 in range(0, 16, 4):
+                mm([((T.key[lo:hi, 15 - k:E:17], ("key", 0, E)), (T.cs[:, 16 * lo + k:16 * hi:16], ("cs", 16 * lo, 16 * hi)), sign[SH[t][lo // 64]], 8)
+                    for k in range(k0, k0 + 4)], first=False, last=False)
 
     def visit(t, a, h):
         q = (r + a) % N
-        win = o("notes", q * SL, q * SL + H)
         nm = lambda n: n + "_%d" % h
-        for c in SUBS:
-            w = c[1] - c[0]
-            offs = o(nm("off"), c[0] // 16, c[1] // 16)
-            if c == SUBS[0]:
-                vgtt(o(nm("cm"), *c), win, offs, o(nm("fvs"), 0, w), OP.is_lt, w)
-                continue
-            agather(o(nm("gx"), *c), win, offs, w)
-            vtt(o(nm("cm"), *c), o(nm("gx"), *c), o(nm("fvx"), 0, w), OP.is_lt, w)
         s64 = lambda n: o(nm(n), 0, 64)
-        acp(s64("sq"), s64("cc"), 64, AF.Square, bias=T.con[:, 0:1])
-        acp(s64("rr"), s64("cc"), 64, AF.Identity, bias=T.con[:, 1:2])
-        vts(s64("vs"), s64("sq"), 1.0 / 32, OP.mult, 64, -13.0 / 32, OP.add)
-        count(o(nm("nn"), 0, 64), nm("cm"))
-        kap = T["kap%d" % t][:, q:q + 1] if t else -8.0
-        vts(o(nm("nn"), 64, 128), o(nm("nn"), 0, 64), float(W), OP.mult, 64, kap, OP.add, sreg=("kap%d" % t, q, q + 1) if t else None)
-        vtt(o(nm("nn"), 128, 192), o(nm("nn"), 64, 128), s64("vs"), OP.add, 64)
-        vtt(s64("qi"), o(nm("nn"), 128, 192), s64("rr"), OP.max, 64)
-        vts(s64("ci"), s64("qi"), 4095, OP.bitwise_and, 64)
+        F, f0 = "F%d" % (t % 2), 1024 * h
+        cv = sum(CV)
+        CA = 64 - cv
+
+        x = {}
+        d, gx = o(nm("df"), 0, 16 * CA), o(nm("gx"), 16 * cv, 1024)
+        mm([(d, IDN, o(F, f0 + 16 * cv, f0 + 1024), 16 * CA)], last=False)
+        x["ga"] = agather(gx, note(q), o(nm("off"), cv, 64), 16 * CA)
+        mm([(d, IDM, gx, 16 * CA)], first=False)
+        x["sg"] = act(o(nm("cm"), 16 * cv, 1024), d, 16 * CA, AF.Sigmoid, con(2), 200.0)
+        cuts = [sum(CV[:i]) for i in range(len(CV) + 1)]
+        x["gv"] = [vgtt(o(nm("cm"), 16 * lo, 16 * hi), note(q), o(nm("off"), lo, hi), o(F, f0 + 16 * lo, f0 + 16 * hi), OP.is_lt, 16 * (hi - lo))
+                   for lo, hi in zip(cuts, cuts[1:])]
+        x["sq"] = act(s64("sq"), s64("cc"), 64, AF.Square, con(0))
+        x["vs"] = act(s64("vs"), s64("sq"), 64, AF.Identity, con(1), (1 + 2.0 ** -22) / 32)
+        kap = con(3) if t == 0 else o("kown", t, t + 1) if a == 0 else o("kap%d" % t, q, q + 1)
+        x["vk"] = act(o(nm("vk"), 1, 128, 2), s64("vs"), 64, AF.Identity, kap)
+        count(o(nm("nn"), 385, 512, 2), nm("cm"))
+        x["small"] = [scan(o(nm("nn"), 128, 256), o(nm("nn"), 384, 512), o(nm("vk"), 0, 128), OP.mult, OP.add, 128),
+                      vtt(s64("qi"), o(nm("nn"), 129, 256, 2), s64("cc"), OP.max, 64),
+                      vts(s64("ci"), s64("qi"), 4095, OP.bitwise_and, 64)]
         if a < N - 1:
-            vcp(s64("off"), s64("ci"), 64)
-            vcp(s64("cc"), s64("ci"), 64)
+            x["small"].append(vcp(s64("off"), s64("ci"), 64))
+            x["cc"] = [vcp(s64("cc"), s64("ci"), 64)]
         else:
-            vts(o(nm("ci"), 64, 128), s64("qi"), 4095, OP.bitwise_and, 64)
+            x["small"].append(vts(o("c16", 64 * h, 64 * h + 64), s64("ci"), -2048.0, OP.add, 64))
+        return x
 
-    def elect(h):
-        nm = lambda n: n + "_%d" % h
-        el = nm("el")
-        vcp(o(el, 0, 128), o(nm("ci"), 0, 128), 128)
-        ee = T[nm("ee")]
+    def weave(slots, takes):
+        row = []
+        for s, x in enumerate(slots):
+            row += (slots[s - 2]["cc"] if s > 1 else []) + takes.get(s, [])
+            small = slots[s - 1]["small"] if s else []
+            k = len(small) - len(x["gv"])
+            row += [i for pair in zip(x["gv"], small[:len(x["gv"])]) for i in pair] + small[len(x["gv"]):] if s else x["gv"]
+        rows_ = [row, [x[n] for x in slots for n in AORD]]
+        for lst in rows_:
+            for u, i in zip(lst, lst[1:]):
+                ops[i]["d"].setdefault(u, False)
+
+    def pairs(h):
+        c = o("c16", 64 * h, 64 * h + 64)
+        for bank, lst in (("df_%d" % h, (1, 2, 3)), ("nn_%d" % h, (4, 5, 6, 7, 8))):
+            place = lambda s: o(bank, 64 * (s - lst[0]), 64 * (s - lst[0]) + 64)
+            for s in lst:
+                mm([(place(s), o("rot", 128 * s - 128, 128 * s), c, 64)])
+            for s in lst:
+                vtt(o("ee", 128 * s - 128 + 64 * h, 128 * s - 64 + 64 * h), place(s), c, OP.is_equal, 64)
+
+    def elect(t):
+        key, dl = o("key", 0, E), o("nn_0", 0, E)
+        mm([(dl, w128("c16"), o("dp", 0, E), E), (dl, w128("c16"), o("dn", 0, E), E)])
         for s in range(1, 9):
-            w = 64 + 4 * s if s < 8 else 64
-            x = (lambda s=s, w=w: V.tensor_tensor(ee[:, s - 1, 0:w], T[nm("ci")][:, 4 * s - (w - 64):4 * s - (w - 64) + w], T[el][:, 128 - w:128], OP.is_equal))
-            add("V", "c", [x], [(nm("ci"), 0, 128), (el, 0, 128)], [(nm("ee"), 96 * s - 96, 96 * s)], w * CY)
-        first = [True]
-        for s in range(1, 9):
-            cols = [0, 4 * s] if s < 8 else [0]
-            for c in cols:
-                st, sp = first[0], s == 8
-                first[0] = False
-                add("P", "c", [lambda s=s, c=c, st=st, sp=sp: PE.matmul(T[nm("nn")][:, 192:256], T.idb[:], ee[:, s - 1, c:c + 64], st, sp)],
-                    [("idb", 0, 128), (nm("ee"), 96 * s - 96, 96 * s)], [(el + "m", 0, 64)], 64 * 0.85)
-        lastm = len(ops) - 1
-        banks[nm("nn")]["P"] = lastm
-        hist[nm("nn")] = hist.get(nm("nn"), []) + [(lastm, 192, 256, True)]
-        kk = T[nm("kk")]
-        K = lambda w: (kk[:, w, :], (nm("kk"), 64 * w, 64 * w + 64))
-        m = o(nm("nn"), 192, 256)
-        vtt(K(0), m, o(nm("shw"), 0, 64), OP.add, 64)
-        vtt(K(1), o(nm("shl"), 0, 64), m, OP.subtract, 64)
-
-        def tree(src, op, dst):
-            w = 64
-            for t in ("t1", "t2", "t3"):
-                w //= 2
-                x, y = T[src], T[nm(t)]
-                vtt((y[:], (nm(t), 0, 99)), (x[:, :, 0:w], (src, 0, 128)), (x[:, :, w:2 * w], (src, 0, 128)), op, 2 * w)
-                src = nm(t)
-            dst(T[src])
-        mx = nm("mx")
-
-        def top(x):
-            for w in range(2):
-                vtt(o(mx, 8 * w, 8 * w + 4), (x[:, w, 0:4], (nm("t3"), 0, 99)), (x[:, w, 4:8], (nm("t3"), 0, 99)), OP.max, 4)
-        tree(nm("kk"), OP.max, top)
+            ee = o("ee", 128 * s - 128, 128 * s)
+            mm([(key, ee, o("rs", E * (s % 8), E * (s % 8) + E), E)], first=False, last=s == 8)
+        half = lambda n, w: o(n, E * w, E * w + E)
+        for w, op in enumerate((OP.max, OP.min)):
+            scan(half("run", w), half("d0", w), key, OP.add, op, E)
         for w in range(2):
-            oh = (T[nm("oh")][:, w, :], (nm("oh"), 64 * w, 64 * w + 64))
-            vgtt(oh, o(mx, 8 * w, 8 * w + 4), o("offx", 0, 4), K(w), OP.is_equal, 64)
-            vtt((T[nm("pp")][:, w, :], (nm("pp"), 64 * w, 64 * w + 64)), oh, o(el, 64, 128), OP.mult, 64)
-
-        def fin(x):
-            vtt((T.val[:, :, 4 * h:4 * h + 4], ("val", 8 * h, 8 * h + 8)), (x[:, :, 0:4], (nm("t3"), 0, 99)), (x[:, :, 4:8], (nm("t3"), 0, 99)), OP.add, 8)
-        tree(nm("pp"), OP.add, fin)
-
-    VALR = ("val", 0, 16)
-
-    def split(w):
-        v = (T.val[:, w, :], VALR)
-        vts(o("hl", 16 * w, 16 * w + 8), v, 4032, OP.bitwise_and, 8)
-        vts(o("hl", 16 * w + 8, 16 * w + 16), v, 63, OP.bitwise_and, 8)
-        vgtt(o("xx", 256 * w, 256 * w + 256), o("hl", 16 * w, 16 * w + 16), o("offq", 0, 16), o("dm", 0, 256), OP.mult, 256)
-
-    def rep(out, w, l0, l1):
-        mms(out, [(l0, o("xx", 256 * w, 256 * w + 128)), (l1, o("xx", 256 * w + 128, 256 * w + 256))], 128)
-
-    BLK = o("blk", 0, 128)
+            vtt(half("nr", w), key, half("run", w), OP.not_equal, E)
+        for w in range(2):
+            scan(half("er", w), dl, half("nr", w), OP.add, OP.mult, E)
 
     def won(t):
-        split(0)
-        if t < ROUNDS - 1:
-            rep(o("el_1", 192, 320), 0, cnt(0), cnt(1))
-            acp(o("hw", P0 + 128 * t, P0 + 128 * t + 128), o("el_1", 192, 320), 128)
+        v, hi, lo = o("er", 16, E, 17), o("hl", 0, 128, 16), o("hl", 1, 128, 16)
+        act(hi, v, 8)
+        vtt(lo, v, hi, OP.subtract, 8)
+        x = o("df_0", 0, 128)
+        mm([(x, w128("hl"), IDN, 128)])
+        act(o("hw", P0 + 128 * t, P0 + 128 * t + 128), x, 128)
 
     def book(t):
-        rep(o("au_0", 128, 256), 0, BLK, BLK)
-        acp(o("yhs", 128 * t, 128 * t + 128), o("au_0", 128, 256), 128)
+        x = o("key", 256, 384)
+        mm([(x, BLK, o("hw", P0 + 128 * t, P0 + 128 * t + 128), 128)])
+        act(o("yhs", 128 * t, 128 * t + 128), x, 128)
         dma("S", "yh%d" % t, T.yh[:, 128 * t:128 * t + 128], T.yhs[0:128:16, 128 * t:128 * t + 128], [("yhs", 128 * t, 128 * t + 128)], [("yh", 128 * t, 128 * t + 128)])
-        if t == ROUNDS - 1:
-            return
-        vcp(o("hlb", 0, 16), o("hl", 0, 16), 16)
-        mms(o("au_1", 128, 144), [(o("ones", 0, 128), o("hlb", 0, 16))], 16)
+
+    def kappa(t):
+        x = o("key", 256, 384)
         ks, ki, kj = o("ks", 0, 1), o("ki", 0, 1), o("kj", 0, 1)
-        add("V", "c", [lambda: V.tensor_reduce(T.ks[:, 0:1], T.au_1[:, 128:144], AxisListType.X, OP.add)], [("au_1", 128, 144)], [("ks", 0, 1)], 64.0)
+        mm([(x, w128("ones"), w128("hl"), 128)])
+        act(w128("kw"), x, 128, acc=ks)
         vcp(ki, ks, 1)
         vts(kj, ki, 255, OP.bitwise_and, 1)
-        vts(o("kap%d" % (t + 1), r, r + 1), kj, -8.0, OP.add, 1)
-        vcp(o("msg%d" % t, 136, 137), kj, 1)
+        vts(o("kown", t + 1, t + 2), kj, KAP0, OP.add, 1)
+        vcp(o("inb%d" % t, r * MS + 136, r * MS + 137), kj, 1)
+
+    def rows():
+        mm([(o("fp_0", 0, 336), IDN, o("ct", 0, 336), 336)], last=False)
+        mm([(o("fp_1", 0, 240), IDN, o("ct", 336, 576), 240)], last=False)
 
     def lost(t):
-        lval = (T.val[:, 1, :], VALR)
-        vcp(o("loff", 0, 8), lval, 8)
-        split(1)
-        vcp(o("lv", 0, 8), lval, 8)
-        rep(o("el_0", 192, 320), 1, BLK, BLK)
-        xo, xc, xn = (o(n, 0, 128) for n in ("xo", "xc", "xn"))
-        fv = o("fe", P0 + 128 * t, P0 + 128 * t + 128)
-        own = r * SL
-        agather(xo, o("notes", own, own + H), o("loff", 0, 8), 128)
-        pd, px = o("nn_0", 256, 384), o("nn_1", 256, 384)
-        mms(pd, [(o("idn", 0, 128), fv), (o("idm", 0, 128), xo)], 128)
+        er, ox = o("er", 0, 2 * E), o("offx", 0, 8)
+        X, Y = o("xy", 0, 128), o("xy", 128, 256)
+        msg = lambda lo, hi: o("inb%d" % t, r * MS + lo, r * MS + hi)
+        vgtt(X, er, ox, w128("dm"), OP.mult, 128)
+        vgather(Y, er, ox, 128)
+        ev = o("nn_1", 256, 264)
+        mm([(ev, X, o("blk", 0, 128, 16), 8), (ev, IDN, o("c21", 0, 8), 8)])
+        vts(o("loff", 0, 8), ev, -float(B), OP.add, 8)
+        place = [o(*ROW[b]) for b in range(8)]
+        for bs in ((0, 1, 2, 3, 4, 5), (6, 7)):
+            mm([(place[b], x, o(n, c * b, c * b + 16 * b + 16), 16 * b + 16) for x, n, c in ((X, "xb", 128), (Y, "idb", 0)) for b in bs], first=False)
+        xo, xc = w128("xo"), w128("xc")
+        agather(xo, note(r), o("loff", 0, 8), 128)
+        pd, px = o("df_1", 0, 128), o("df_1", 128, 256)
+        mm([(pd, IDN, goods(t), 128), (pd, IDM, xo, 128)])
         for b in range(8):
-            w = 16 * b + 16
-            vts((T.eq[:, b, 128 - w:128], ("eq", 128 * b, 128 * b + 128)), (T.el_0[:, 192:192 + w], ("el_0", 192, 320)), T.lv[:, b:b + 1], OP.is_equal, w, sreg=("lv", 0, 8))
-        dg = (T.eq[:, :, 112:128], ("eq", 0, 1024))
-        vtt(dg, dg, (T.dt[:], ("dt", 0, 128)), OP.mult, 128)
-        for b in range(8):
-            w = 16 * b + 16
-            add("V", "c", [lambda b=b, w=w: V.tensor_reduce(T.dd[:, b:b + 1], T.eq[:, b, 128 - w:128], AxisListType.X, OP.max)], [("eq", 128 * b, 128 * b + 128)], [("dd", b, b + 1)], max(64, w) * CY)
+            add("V", "c", [lambda b=b: V.tensor_reduce(T.dd[:, b:b + 1], place[b][0], AxisListType.X, OP.min, apply_absolute_value=True)],
+                [place[b][1]], [("dd", b, b + 1)], max(64, 16 * b + 16) * CY)
         vts(xc, pd, 32.0, OP.min, 128, -32.0, OP.max)
-        mms(px, [(o("idn", 0, 128), xo), (o("idn", 0, 128), xc)], 128)
-        acp(xn, px, 128)
-        vtt(o("d1", 0, 8), o("dd", 0, 8), o("md", 0, 8), OP.mult, 8)
-        vtt(o("d2", 0, 8), o("d1", 0, 8), o("lv", 0, 8), OP.max, 8)
-        oo = o("msg%d" % t, 0, 8) if t < ROUNDS - 1 else o("loff", 0, 8)
-        vcp(oo, o("d2", 0, 8), 8)
-        add("V", "c", [lambda: V.tensor_copy(T.notes[:, own:own + SL].indirect(oo[0]), xn[0])], [xn[1], oo[1]], [("notes", own, own + SL)], 50 + 128 * 3.0)
+        vtt(o("d1", 0, 8), ev, o("dd", 0, 8), OP.min, 8)
+        vcp(msg(0, 8), o("d1", 0, 8), 8)
+        add("V", "c", [lambda: V.tensor_tensor(slot(r)[0].indirect(msg(0, 8)[0]), xo[0], xc[0], OP.add)], [xo[1], xc[1], msg(0, 8)[1]], [slot(r)[1]], 50 + 128 * SC * CY)
         if t < ROUNDS - 1:
-            vcp(o("msg%d" % t, 8, 136), xn, 128)
+            mm([(px, IDN, xo, 128), (px, IDN, xc, 128)])
+            vcp(msg(8, 136), px, 128)
 
     def send(t):
-        m = "msg%d" % t
-        fill(m, 137, MS, 0)
+        m = o("inb%d" % t, r * MS, r * MS + MS)
         others = [T.cores[(r - a) % N] for a in range(1, N)]
         mask = topo.mask(core, others[0])
 
         def fn():
             ids = [DstId(rid=topo.addr(c)[0], pnc=topo.addr(c)[1]) for c in others]
-            dst = T["inb%d" % t][:, r * MS:r * MS + MS]
             return g.remote_dma_fused([RemoteDMATransfer(dst_ids=ids, dma_engine_mask=mask, remote_sem=T.sem["m%d_%d" % (t, r)],
-                                                         srcs=[T[m][:]], dsts=[dst for c in ids], alu_op=0)], local_sem=T.sem.msem)
+                                                         srcs=[m[0]], dsts=[m[0] for c in ids], alu_op=0)], local_sem=T.sem.msem)
         ne = len(topo.engines(core, others[0]))
-        s = add("G", "r", [fn], [(m, 0, MS)], [], 1000.0, name=("msem", ne))
+        s = add("G", "r", [fn], [m[1]], [], 1000.0, name=("msem", ne))
         for a in range(1, N):
             q = (r + a) % N
             add("X", "a", [], [], [("inb%d" % t, q * MS, q * MS + MS)], 2500.0, ("m%d_%d" % (t, q), ne), extra=[s])
@@ -411,47 +470,86 @@ def build(g, r, T, topo):
         q = (r + a) % N
         inb = "inb%d" % t
         x = T[inb]
-        add("V", "c", [lambda: V.tensor_copy(T.notes[:, q * SL:q * SL + SL].indirect(x[:, q * MS:q * MS + 8]), x[:, q * MS + 8:q * MS + 136])],
-            [(inb, q * MS, q * MS + MS)], [("notes", q * SL, q * SL + SL)], 50 + 128 * 3.0)
-        vts(o("kap%d" % (t + 1), q, q + 1), o(inb, q * MS + 136, q * MS + 137), -8.0, OP.add, 1)
+        w = 8 // TP
+        name = slot(q)[1][0]
+        before, done = list(hist[name]), []
+        for j in range(0, 8, w):
+            hist[name] = list(before)
+            c = q * MS + 8 + 16 * j
+            i = add("V", "c", [lambda j=j, c=c: V.tensor_copy(slot(q)[0].indirect(x[:, q * MS + j:q * MS + j + w]), x[:, c:c + 16 * w])],
+                    [(inb, q * MS, q * MS + MS)], [slot(q)[1]], 50 + 16 * w * SC * CY)
+            if done:
+                ops[i]["d"][done[-1][0]] = True
+            done.append((i, q * SL, q * SL + SL, True))
+        hist[name] = [z for z in hist[name] if z[0] != done[-1][0]] + done
+        if a == 1:
+            vts(o("kap%d" % (t + 1), 0, N), (x[:, 136:N * MS:MS], (inb, 0, N * MS)), KAP0, OP.add, N)
+        return [z[0] for z in done]
 
     for t in range(ROUNDS):
         for h in range(2):
+            if t == 0:
+                fill(o("nn_%d" % h, 384, 512), 0.0, 128)
+                fill(o("vk_%d" % h, 0, 128), float(W), 128)
+            late[1] = AHEAD * (1 - h)
             heads(t, h)
-        for h in range(2):
-            fvx(t, h)
+            late[1] = 0.0
+        if t:
+            book(t - 1)
+        slots, takes = [], {}
         for a in range(N):
             if t and a:
-                take(t - 1, a)
+                for j, i in enumerate(take(t - 1, a)):
+                    if a > 1:
+                        takes.setdefault(2 * a - 2 + 2 * j // TP if TP > 1 else 2 * a - 1, []).append(i)
             for h in range(2):
-                visit(t, a, h)
+                late[1] = AHEAD * (1 - h)
+                slots.append(visit(t, a, h))
+                late[1] = 0.0
+                if a == N - 1:
+                    pairs(h)
+            late[0] = True
             if t == 0 and a == 0:
                 tables()
-            if a in (SHARE_AT, SHARE_AT + 1):
-                shares(t, a - SHARE_AT)
-            if a == 2 and t < ROUNDS - 1:
-                convert(t + 1)
-        for h in range(2):
-            elect(h)
+                for u in range(ROUNDS - 1):
+                    fill(o("inb%d" % u, r * MS + 137, r * MS + MS), 0)
+            if a == 0 and t < ROUNDS - 1:
+                spread(t + 1)
+            if a == 1:
+                shares(t, 0, 1)
+                keys(t)
+            late[0] = False
+        weave(slots, takes)
+        rows()
+        elect(t)
+        won(t)
+        lost(t)
         if t < ROUNDS - 1:
-            won(t)
-            lost(t)
-            book(t)
+            kappa(t)
             send(t)
-        else:
-            lost(t)
-            won(t)
-            book(t)
-    dma("S", "yl", T.yl[:], T.notes[:, r * SL:r * SL + H], [("notes", r * SL, r * SL + H)], [("yl", 0, 1)], 5000.0)
+    book(ROUNDS - 1)
+    dma("S", "yl", T.yl[:], note(r)[0], [note(r)[1]], [("yl", 0, 1)], 5500.0)
     return ops
 
 
 def order(ops):
     n = len(ops)
+    hop = TIMES["hop"]
     succ = [[] for _ in range(n)]
     for i, x in enumerate(ops):
         for u in x["d"]:
             succ[u].append(i)
+    left = [len(x["d"]) for x in ops]
+    serial = [i for i in range(n) if not left[i]]
+    for i in serial:
+        for j in succ[i]:
+            left[j] -= 1
+            if not left[j]:
+                serial.append(j)
+    tail = [0.0] * n
+    for i in reversed(serial):
+        tail[i] = ops[i]["t"] + max([(hop if ops[j]["d"][i] else 0.0) + tail[j] for j in succ[i]] + [0.0])
+    urge = lambda j: (tail[j] + ops[j]["u"] + (EARLY if ops[j]["late"] else 0.0), -j)
     missing = [len(x["d"]) for x in ops]
     avail = [0.0] * n
     ready = {}
@@ -468,7 +566,16 @@ def order(ops):
                 continue
             f = 0.0 if e == "X" else free.get(e, 0.0)
             t0 = min(max(f, avail[i]) for i in lst)
-            i = min(j for j in lst if max(f, avail[j]) <= t0 + 1e-6)
+            now = [j for j in lst if max(f, avail[j]) <= t0 + 1e-6]
+            i = max(now, key=urge)
+            soon = [j for j in lst if t0 < avail[j] <= t0 + SLACK[ops[i]["late"]] and urge(j) > urge(i)]
+            if soon and e != "X":
+                j = max(soon, key=urge)
+                fit = [k for k in now if t0 + ops[k]["t"] <= avail[j] + 20]
+                if fit:
+                    i = max(fit, key=urge)
+                else:
+                    i, t0 = j, avail[j]
             if best is None or t0 < best[0]:
                 best = (t0, i, e)
         t0, i, e = best
@@ -479,7 +586,7 @@ def order(ops):
         free[e] = t0 + (60.0 if x["k"] == "d" else x["t"])
         seq.append(i)
         for j in succ[i]:
-            avail[j] = max(avail[j], end + HOP)
+            avail[j] = max(avail[j], end + (hop if ops[j]["d"][i] else 0.0))
             missing[j] -= 1
             if not missing[j]:
                 ready.setdefault(ops[j]["e"], []).append(j)
@@ -508,7 +615,7 @@ def rank_program(g, core, T, topo):
         kn = known[e]
         need = {}
         for u, raw in x["d"].items():
-            if ops[u]["e"] == e and ops[u]["k"] == "c" and x["k"] == "c" and not raw:
+            if not raw:
                 continue
             s, c = key[u]
             if kn.get(s, 0) < c:

@@ -4,32 +4,35 @@ from concourse.mybir import AluOpType as OP, AxisListType, ActivationFunctionTyp
 N = 8
 H, P0, B, ROUNDS = 4096, 1536, 128, 4
 SL = B + H
-W = 613 + 4096 * 129
+W = 613 + 4096 * 228
 R = (9 * W // 4096) * 4096
-M23 = 2.0 ** 23
-KAP0 = -8.0 - R - M23
+KAP0 = -8.0 - 13.0 / 32
 BIG = 2.0 ** 18
 MS = 144
 E = 136
-ROW = [("fp_0", 8 * b * (b + 1), 8 * (b + 1) * (b + 2)) if b < 6 else ("fp_1", 112 * (b - 6), 112 * (b - 6) + 16 * b + 16) for b in range(8)]
+CT = [8 * b * (b + 1) + b for b in range(9)]
+CUT = 5
 
-CV = (20, 8, 8, 8)
-AORD = ("ga", "sq", "vs", "sg", "vk")
-SH = ("AA", "AA", "AA", "AA")
-SLACK = (100.0, 300.0)
-EARLY = 4000.0
-TP = 2
+SPLIT = {0: ((46,), 18), 15: ((50,), 14), "else": ((22, 8, 8), 14)}
+AORD = ("ga0", "ga1", "sq", "sg0", "sg1", "vk")
+SH = ("VVVA", "AAAV", "AAAV", "AAAV")
+SW = (512, 512, 512, 256)
+BETWEEN = ("max0 sv0 and0 scan1 end0 max1 end1 sv1", "X lo Y loff ks hv00 ki r7 r6 r5 kj cut r4 r3 r2 r1 r0 km list new hv10 put off0 cc0 hv11",
+           "vk1 sg0 sg1 sr0 sg2 sr1 hi hw xo ha0 ha1", "sp0 rot01 rot18 step key8 sp1", "ev turn sum x5 y5 x0 y0 pd")
+LAST = ("X Y loff r7 r6 r5 lo r4 r3 r2 r1 r0 list cut put", "ev x5 y5 x0 y0 pd turn")
+SLACK = (150.0, 450.0)
+EARLY = 3000.0
+TP, T1 = 4, 1
+FV = 0
 AHEAD = 1500.0
-HV = (32, 16)
-WN = "A"
-SP = 256
+HV = (((32,), (32,)), ((8,), (12,)))
 
 SCRATCH = {"notes": ("sbuf", [128, N * SL], "bfloat16")}
 for _d, _l in (("bfloat16", (("fe", 2048), ("hw", 2048), ("cnt", 2048), ("F0", 2048), ("F1", 2048), ("cs", 2048), ("gs", 1024), ("hdb", 192),
                              ("dm", 128), ("dmp", 128), ("blk", 128), ("nblk", 8), ("vv", 128), ("vt", 128), ("idn", 128), ("idm", 128), ("idb", 128),
                              ("ones", 128), ("xo", 128), ("xc", 128), ("hl", 128), ("rv", 128), ("rot", 1024), ("ee", 1024), ("xb", 1024),
                              ("jc", E), ("gcol", E), ("ofb", E), ("za", E), ("zb", E), ("zm", E), ("zr", E), ("rs", 8 * E), ("dp", E), ("dn", E),
-                             ("d0", 2 * E), ("nr", 2 * E), ("zer", E), ("pen", 16), ("c21", 8), ("ct", 576))),
+                             ("d0", 2 * E), ("nr", 2 * E), ("zer", E), ("pen", 16), ("c21", 8), ("ct", CT[8]))),
                ("float16", (("c16", 128), ("xy", 256))),
                ("int32", (("ci0", 512), ("hdi", 96), ("hdx", 192), ("ia", 128), ("ib", 128), ("ja", 128), ("jb", 128), ("ka", 128), ("kb", 128),
                           ("iu", 128), ("iz", E), ("ix", 8), ("ki", 1), ("kj", 1))),
@@ -55,13 +58,14 @@ DMAS = ["comp0", "comp1", "hd", "fe0", "fe1", "lim", "hwa", "hwb", "yh0", "yh1",
 SEMAPHORES = (["pV", "pA", "pP", "pG", "lsem", "msem"] + ["d_" + n for n in DMAS] + ["lim%d" % q for q in range(N)]
               + ["m%d_%d" % (t, q) for t in range(ROUNDS - 1) for q in range(N)])
 
-TIMES = {"cy": 1.0, "pe": 0.5, "hop": 215.0, "gather": 1.5, "scatter": 3.5, "note": 4000.0}
+TIMES = {"cy": 0.95, "pe": 0.5, "hop": 210.0, "gather": 1.5, "scatter": 3.5, "note": 3700.0}
 
 
 def build(g, r, T, topo):
     ops = []
     hist = {}
     banks = {}
+    at, turns = {}, {}
     core = T.cores[r]
     V, A, PE, S = g.vector, g.scalar, g.tensor, g.sync
     CY, PC, GA, SC = (TIMES[n] for n in ("cy", "pe", "gather", "scatter"))
@@ -175,8 +179,6 @@ def build(g, r, T, topo):
     dma("S", "hd", T.hdi[:], T.hd[:], [], [("hdi", 0, 96)])
     dma("S", "comp0", T.ci0[:, 0:128], T.comp[:, 0:128], [], [("ci0", 0, 128)])
     dma("S", "fe1", T.fe[:, P0:2048], T.feat[:, P0:2048], [], [("fe", P0, 2048)], 3000.0)
-    dma("S", "fe0", T.fe[:, 0:P0], T.feat[:, 0:P0], [], [("fe", 0, P0)], 5000.0)
-    dma("S", "comp1", T.ci0[:, 128:512], T.comp[:, 128:512], [], [("ci0", 128, 512)], 5000.0)
 
     def iota(name, w, pat, base, ch):
         out = T[name]
@@ -193,7 +195,7 @@ def build(g, r, T, topo):
     iota("gcol", E, [[1, 8], [0, 17]], 0, 0)
     iota("ix", 8, [[17, 8]], E + 16, 0)
     zeros = fill(o("hw", 0, 2048), 0.0, 2048)
-    for i, v in enumerate((16.0, M23 - 0.5, -100.0, KAP0)):
+    for i, v in enumerate((16.0 - R, float(R), -100.0, KAP0)):
         fill(con(i), v)
     vts(o("hdx", 0, 96), o("hdi", 0, 96), 4032, OP.bitwise_and, 96)
     vts(o("hdx", 96, 192), o("hdi", 0, 96), 63, OP.bitwise_and, 96)
@@ -204,6 +206,9 @@ def build(g, r, T, topo):
     i2 = dma("S", "hwb", T.hw[1:128:16, 0:P0], T.hdb[:, 96:192], [("hdb", 96, 192)], [("hw", 0, P0)])
     ops[i2]["d"][zeros] = True
     hist["hw"] = keep + [(i2, 0, P0, True)]
+    i3 = dma("S", "fe0", T.fe[:, 0:P0], T.feat[:, 0:P0], [], [("fe", 0, P0)], 4000.0)
+    i4 = dma("S", "comp1", T.ci0[:, 128:512], T.comp[:, 128:512], [], [("ci0", 128, 512)], 4000.0)
+    ops[i3]["d"][i2] = ops[i4]["d"][i3] = False
     vts(w128("ja"), w128("ia"), 4, OP.arith_shift_right, 128)
     vts(w128("jb"), w128("ib"), 4, OP.arith_shift_right, 128)
     vts(w128("ka"), w128("ia"), 15, OP.bitwise_and, 128)
@@ -224,8 +229,10 @@ def build(g, r, T, topo):
         for k in range(16):
             hist[name] = list(keep)
             out = (T[name][:, k:2048:16], (name, 0, 2048))
-            if t == 0:
+            if t == 0 and k < FV:
                 vcp(out, goods(t), 128)
+            elif t == 0:
+                act(out, goods(t), 128)
             else:
                 select(out, goods(t), [[0, 128]], 0, 0, 128)
             done.append((len(ops) - 1, 0, 2048, True))
@@ -255,7 +262,6 @@ def build(g, r, T, topo):
         vts(w128("dmp"), w128("dm"), col(2), OP.mult, 128)
         vts(IDB, IDN, -8192.0, OP.mult, 128)
         fill(w128("ones"), 1.0)
-        fill(o("c21", 0, 8), 2048.0 + B)
         fill(w128("hl"), 0.0)
         fill(o("hl", 2, 128, 16), 2048.0)
         vcp(o("offx", 0, 8), o("ix", 0, 8), 8)
@@ -286,47 +292,58 @@ def build(g, r, T, topo):
         select(xb, xb, [[-16, 8], [0, 128]], 0, 1, 1024)
         select(xb, xb, [[16, 8], [0, 128]], 15, -1, 1024)
         for s in range(1, 8):
-            x = o("sh", 0, E)
+            x = o("key", 0, E)
             mm([(x, IDN, o("rs", E * s, E * s + E), E), (x, IDN, o("rs", 0, E), E)])
             act(o("rs", E * s, E * s + E), x, E)
+        fill(o("ct", 0, CT[8]), 2048.0 + B, CT[8])
         for b in range(8):
-            w, c = 16 * b + 16, 8 * b * (b + 1)
-            x = o("sh", 0, w)
-            mm([(x, w128("dmp"), o("xb", 128 * b, 128 * b + w), w), (o("sh", w - 16, w), IDB, o("pen", 0, 16), 16)])
+            w, c = 16 * b + 16, CT[b]
+            x = o("key", 0, w)
+            mm([(x, w128("dmp"), o("xb", 128 * b, 128 * b + w), w), (o("key", w - 16, w), IDB, o("pen", 0, 16), 16)])
             act(o("ct", c, c + w), x, w)
 
     def heads(t, h):
         oc = 128 * t + 64 * h
-        cv = HV[min(t, 1)]
         gx, hw = "gx_%d" % h, o("hw", 0, 2048)
-        if cv:
-            vgather(o(gx, 0, 16 * cv), hw, o("offc", oc, oc + cv), 16 * cv)
-        agather(o(gx, 16 * cv, 1024), hw, o("offc", oc + cv, oc + 64), 1024 - 16 * cv)
+        cv = 0
+        for j, w in enumerate(HV[min(t, 1)][h]):
+            at["hv%d%d" % (h, j)] = vgather(o(gx, 16 * cv, 16 * (cv + w)), hw, o("offc", oc + cv, oc + cv + w), 16 * w)
+            cv += w
+        at["ha%d" % h] = agather(o(gx, 16 * cv, 1024), hw, o("offc", oc + cv, oc + 64), 1024 - 16 * cv)
         out = o("nn_%d" % h, 0, 64)
         count(out, gx)
-        vcp(o("off_%d" % h, 0, 64), out, 64)
-        act(o("cc_%d" % h, 0, 64), out, 64)
+        at["off%d" % h] = vcp(o("off_%d" % h, 0, 64), out, 64)
+        at["cc%d" % h] = vts(o("cc_%d" % h, 0, 64), out, float(R), OP.add, 64)
 
-    def shares(t, part, parts):
-        n = 2048 // SP
+    def shares(t, takes):
         F = "F%d" % (t % 2)
-        for s in range(n * part // parts, n * (part + 1) // parts):
-            c = SP * s
-            gs, d = o("gs", c % 1024, c % 1024 + SP), o("sh", c % 512, c % 512 + SP)
-            offs = o("offc", 128 * t + c // 16, 128 * t + (c + SP) // 16)
-            if SH[t][c // 1024] == "V":
-                vgtt(o("cs", c, c + SP), o("fe", 0, 2048), offs, o(F, c, c + SP), OP.min, SP)
-                continue
-            agather(gs, o("fe", 0, 2048), offs, SP)
-            mm([(d, IDN, o(F, c, c + SP), SP), (d, IDM, gs, SP)])
-            act(o("cs", c, c + SP), d, SP, AF.Relu)
+        fe = o("fe", 0, 2048)
+        offs = lambda c, w: o("offc", 128 * t + c // 16, 128 * t + (c + w) // 16)
+        for j in range(4):
+            w = (128 if SH[t][j] == "V" else 256) if t == 0 else SW[j]
+            for c in range(512 * j, 512 * j + 512, w):
+                if SH[t][j] == "V":
+                    i = at["sv%d" % (c // w % 2)] = vgtt(o("cs", c, c + w), fe, offs(c, w), o(F, c, c + w), OP.min, w)
+                    if t == 0:
+                        takes[len(takes) + 2] = [i]
+                    continue
+                gs, d = o("gs", c % 1024, c % 1024 + w), o("sh", 0, w)
+                at["sg%d" % j] = agather(gs, fe, offs(c, w), w)
+                at["sp%d" % j] = mm([(d, IDN, o(F, c, c + w), w), (d, IDM, gs, w)])
+                at["sr%d" % j] = act(o("cs", c, c + w), d, w, AF.Relu)
+
+    def chain(names):
+        lst = [at[n] for n in names.split() if n in at]
+        for u, i in zip(lst, lst[1:]):
+            ops[i]["d"].setdefault(u, False)
 
     def keys(t):
         sign = {"V": o("blk", 0, 128, 16), "A": o("nblk", 0, 8)}
         mm([(o("key", 0, E), IDN, o("zer", 0, E), E)], last=False)
-        for lo, hi in ((0, 128),) if SH[t][0] == SH[t][1] else ((0, 64), (64, 128)):
+        cuts = [0] + [32 * j for j in range(1, 4) if SH[t][j] != SH[t][j - 1]] + [128]
+        for lo, hi in zip(cuts, cuts[1:]):
             for k0 in range(0, 16, 4):
-                mm([((T.key[lo:hi, 15 - k:E:17], ("key", 0, E)), (T.cs[:, 16 * lo + k:16 * hi:16], ("cs", 16 * lo, 16 * hi)), sign[SH[t][lo // 64]], 8)
+                mm([((T.key[lo:hi, 15 - k:E:17], ("key", 0, E)), (T.cs[:, 16 * lo + k:16 * hi:16], ("cs", 16 * lo, 16 * hi)), sign[SH[t][lo // 32]], 8)
                     for k in range(k0, k0 + 4)], first=False, last=False)
 
     def visit(t, a, h):
@@ -334,29 +351,30 @@ def build(g, r, T, topo):
         nm = lambda n: n + "_%d" % h
         s64 = lambda n: o(nm(n), 0, 64)
         F, f0 = "F%d" % (t % 2), 1024 * h
+        CV, CA = SPLIT.get(2 * a + h, SPLIT["else"])
         cv = sum(CV)
-        CA = 64 - cv
-
         x = {}
-        d, gx = o(nm("df"), 0, 16 * CA), o(nm("gx"), 16 * cv, 1024)
-        mm([(d, IDN, o(F, f0 + 16 * cv, f0 + 1024), 16 * CA)], last=False)
-        x["ga"] = agather(gx, note(q), o(nm("off"), cv, 64), 16 * CA)
-        mm([(d, IDM, gx, 16 * CA)], first=False)
-        x["sg"] = act(o(nm("cm"), 16 * cv, 1024), d, 16 * CA, AF.Sigmoid, con(2), 200.0)
+        for j, bank, lo, hi in ((0, "df", cv, cv + CA), (1, "fp", cv + CA, 64)):
+            w = 16 * (hi - lo)
+            if w:
+                d, gx = o(nm(bank), 0, w), o(nm("gx"), 16 * lo, 16 * hi)
+                mm([(d, IDN, o(F, f0 + 16 * lo, f0 + 16 * hi), w)], last=False)
+                x["ga%d" % j] = agather(gx, note(q), o(nm("off"), lo, hi), w)
+                mm([(d, IDM, gx, w)], first=False)
+                x["sg%d" % j] = act(o(nm("cm"), 16 * lo, 16 * hi), d, w, AF.Sigmoid, con(2), 200.0)
         cuts = [sum(CV[:i]) for i in range(len(CV) + 1)]
         x["gv"] = [vgtt(o(nm("cm"), 16 * lo, 16 * hi), note(q), o(nm("off"), lo, hi), o(F, f0 + 16 * lo, f0 + 16 * hi), OP.is_lt, 16 * (hi - lo))
                    for lo, hi in zip(cuts, cuts[1:])]
         x["sq"] = act(s64("sq"), s64("cc"), 64, AF.Square, con(0))
-        x["vs"] = act(s64("vs"), s64("sq"), 64, AF.Identity, con(1), (1 + 2.0 ** -22) / 32)
         kap = con(3) if t == 0 else o("kown", t, t + 1) if a == 0 else o("kap%d" % t, q, q + 1)
-        x["vk"] = act(o(nm("vk"), 1, 128, 2), s64("vs"), 64, AF.Identity, kap)
+        x["vk"] = act(o(nm("vk"), 1, 128, 2), s64("sq"), 64, AF.Identity, kap, 1.0 / 32)
         count(o(nm("nn"), 385, 512, 2), nm("cm"))
         x["small"] = [scan(o(nm("nn"), 128, 256), o(nm("nn"), 384, 512), o(nm("vk"), 0, 128), OP.mult, OP.add, 128),
                       vtt(s64("qi"), o(nm("nn"), 129, 256, 2), s64("cc"), OP.max, 64),
                       vts(s64("ci"), s64("qi"), 4095, OP.bitwise_and, 64)]
         if a < N - 1:
             x["small"].append(vcp(s64("off"), s64("ci"), 64))
-            x["cc"] = [vcp(s64("cc"), s64("ci"), 64)]
+            x["cc"] = [vts(s64("cc"), s64("ci"), float(R), OP.add, 64)]
         else:
             x["small"].append(vts(o("c16", 64 * h, 64 * h + 64), s64("ci"), -2048.0, OP.add, 64))
         return x
@@ -364,11 +382,14 @@ def build(g, r, T, topo):
     def weave(slots, takes):
         row = []
         for s, x in enumerate(slots):
-            row += (slots[s - 2]["cc"] if s > 1 else []) + takes.get(s, [])
-            small = slots[s - 1]["small"] if s else []
-            k = len(small) - len(x["gv"])
-            row += [i for pair in zip(x["gv"], small[:len(x["gv"])]) for i in pair] + small[len(x["gv"]):] if s else x["gv"]
-        rows_ = [row, [x[n] for x in slots for n in AORD]]
+            row += slots[s - 2]["cc"] if s > 1 else []
+            fill_ = [[i] for i in x["gv"]]
+            extra = takes.get(s, [])
+            row += extra[:-1]
+            fill_ += [[]] * (3 - len(fill_)) + [extra[-1:]]
+            for j in range(4):
+                row += fill_[j] + (slots[s - 1]["small"][j:j + 1] if s else [])
+        rows_ = [row, [x[n] for x in slots for n in AORD if n in x]]
         for lst in rows_:
             for u, i in zip(lst, lst[1:]):
                 ops[i]["d"].setdefault(u, False)
@@ -378,16 +399,16 @@ def build(g, r, T, topo):
         for bank, lst in (("df_%d" % h, (1, 2, 3)), ("nn_%d" % h, (4, 5, 6, 7, 8))):
             place = lambda s: o(bank, 64 * (s - lst[0]), 64 * (s - lst[0]) + 64)
             for s in lst:
-                mm([(place(s), o("rot", 128 * s - 128, 128 * s), c, 64)])
+                turns["rot%d%d" % (h, s)] = mm([(place(s), o("rot", 128 * s - 128, 128 * s), c, 64)])
             for s in lst:
-                vtt(o("ee", 128 * s - 128 + 64 * h, 128 * s - 64 + 64 * h), place(s), c, OP.is_equal, 64)
+                turns["eq%d%d" % (h, s)] = vtt(o("ee", 128 * s - 128 + 64 * h, 128 * s - 64 + 64 * h), place(s), c, OP.is_equal, 64)
 
     def elect(t):
         key, dl = o("key", 0, E), o("nn_0", 0, E)
-        mm([(dl, w128("c16"), o("dp", 0, E), E), (dl, w128("c16"), o("dn", 0, E), E)])
+        at["step"] = mm([(dl, w128("c16"), o("dp", 0, E), E), (dl, w128("c16"), o("dn", 0, E), E)])
         for s in range(1, 9):
             ee = o("ee", 128 * s - 128, 128 * s)
-            mm([(key, ee, o("rs", E * (s % 8), E * (s % 8) + E), E)], first=False, last=s == 8)
+            at["key%d" % s] = mm([(key, ee, o("rs", E * (s % 8), E * (s % 8) + E), E)], first=False, last=s == 8)
         half = lambda n, w: o(n, E * w, E * w + E)
         for w, op in enumerate((OP.max, OP.min)):
             scan(half("run", w), half("d0", w), key, OP.add, op, E)
@@ -398,11 +419,11 @@ def build(g, r, T, topo):
 
     def won(t):
         v, hi, lo = o("er", 16, E, 17), o("hl", 0, 128, 16), o("hl", 1, 128, 16)
-        act(hi, v, 8)
-        vtt(lo, v, hi, OP.subtract, 8)
+        at["hi"] = act(hi, v, 8)
+        at["lo"] = vtt(lo, v, hi, OP.subtract, 8)
         x = o("df_0", 0, 128)
-        mm([(x, w128("hl"), IDN, 128)])
-        act(o("hw", P0 + 128 * t, P0 + 128 * t + 128), x, 128)
+        at["turn"] = mm([(x, w128("hl"), IDN, 128)])
+        at["hw"] = act(o("hw", P0 + 128 * t, P0 + 128 * t + 128), x, 128)
 
     def book(t):
         x = o("key", 256, 384)
@@ -413,43 +434,46 @@ def build(g, r, T, topo):
     def kappa(t):
         x = o("key", 256, 384)
         ks, ki, kj = o("ks", 0, 1), o("ki", 0, 1), o("kj", 0, 1)
-        mm([(x, w128("ones"), w128("hl"), 128)])
-        act(w128("kw"), x, 128, acc=ks)
-        vcp(ki, ks, 1)
-        vts(kj, ki, 255, OP.bitwise_and, 1)
+        at["sum"] = mm([(x, w128("ones"), w128("hl"), 128)])
+        at["ks"] = add("V", "c", [lambda: V.tensor_reduce(ks[0], x[0], AxisListType.X, OP.add)], [x[1]], [ks[1]], 128 * CY)
+        at["ki"] = vcp(ki, ks, 1)
+        at["kj"] = vts(kj, ki, 255, OP.bitwise_and, 1)
         vts(o("kown", t + 1, t + 2), kj, KAP0, OP.add, 1)
-        vcp(o("inb%d" % t, r * MS + 136, r * MS + 137), kj, 1)
+        at["km"] = vcp(o("inb%d" % t, r * MS + 136, r * MS + 137), kj, 1)
 
     def rows():
-        mm([(o("fp_0", 0, 336), IDN, o("ct", 0, 336), 336)], last=False)
-        mm([(o("fp_1", 0, 240), IDN, o("ct", 336, 576), 240)], last=False)
+        for bank, lo, hi in (("fp_0", 0, CT[CUT]), ("fp_1", CT[CUT], CT[8])):
+            mm([(o(bank, 0, hi - lo), IDN, o("ct", lo, hi), hi - lo)], last=False)
 
     def lost(t):
         er, ox = o("er", 0, 2 * E), o("offx", 0, 8)
         X, Y = o("xy", 0, 128), o("xy", 128, 256)
         msg = lambda lo, hi: o("inb%d" % t, r * MS + lo, r * MS + hi)
-        vgtt(X, er, ox, w128("dm"), OP.mult, 128)
-        vgather(Y, er, ox, 128)
+        at["X"] = vgtt(X, er, ox, w128("dm"), OP.mult, 128)
+        at["Y"] = vgather(Y, er, ox, 128)
         ev = o("nn_1", 256, 264)
-        mm([(ev, X, o("blk", 0, 128, 16), 8), (ev, IDN, o("c21", 0, 8), 8)])
-        vts(o("loff", 0, 8), ev, -float(B), OP.add, 8)
-        place = [o(*ROW[b]) for b in range(8)]
-        for bs in ((0, 1, 2, 3, 4, 5), (6, 7)):
-            mm([(place[b], x, o(n, c * b, c * b + 16 * b + 16), 16 * b + 16) for x, n, c in ((X, "xb", 128), (Y, "idb", 0)) for b in bs], first=False)
+        at["ev"] = mm([(ev, X, o("blk", 0, 128, 16), 8)])
+        at["loff"] = vts(o("loff", 0, 8), ev, 2048.0, OP.add, 8)
+        part = lambda b, lo, hi: o("fp_%d" % (b >= CUT), CT[b] - CT[CUT] * (b >= CUT) + lo, CT[b] - CT[CUT] * (b >= CUT) + hi)
+        place = [part(b, 0, 16 * b + 17) for b in range(8)]
+        banks_ = (range(CUT, 8), range(CUT))
+        for bs in banks_:
+            at["x%d" % bs[0]] = mm([(part(b, 0, 16 * b + 16), X, o("xb", 128 * b, 128 * b + 16 * b + 16), 16 * b + 16) for b in bs]
+                                   + [(part(b, 16 * b + 16, 16 * b + 17), X, o("blk", 16 * b, 16 * b + 1), 1) for b in bs], first=False, last=False)
+            at["y%d" % bs[0]] = mm([(part(b, 0, 16 * b + 16), Y, o("idb", 0, 16 * b + 16), 16 * b + 16) for b in bs], first=False)
         xo, xc = w128("xo"), w128("xc")
-        agather(xo, note(r), o("loff", 0, 8), 128)
+        at["xo"] = agather(xo, note(r), o("loff", 0, 8), 128)
         pd, px = o("df_1", 0, 128), o("df_1", 128, 256)
-        mm([(pd, IDN, goods(t), 128), (pd, IDM, xo, 128)])
-        for b in range(8):
-            add("V", "c", [lambda b=b: V.tensor_reduce(T.dd[:, b:b + 1], place[b][0], AxisListType.X, OP.min, apply_absolute_value=True)],
-                [place[b][1]], [("dd", b, b + 1)], max(64, 16 * b + 16) * CY)
-        vts(xc, pd, 32.0, OP.min, 128, -32.0, OP.max)
-        vtt(o("d1", 0, 8), ev, o("dd", 0, 8), OP.min, 8)
-        vcp(msg(0, 8), o("d1", 0, 8), 8)
-        add("V", "c", [lambda: V.tensor_tensor(slot(r)[0].indirect(msg(0, 8)[0]), xo[0], xc[0], OP.add)], [xo[1], xc[1], msg(0, 8)[1]], [slot(r)[1]], 50 + 128 * SC * CY)
+        at["pd"] = mm([(pd, IDN, goods(t), 128), (pd, IDM, xo, 128)])
+        for b in reversed(range(8)):
+            at["r%d" % b] = add("V", "c", [lambda b=b: V.tensor_reduce(T.dd[:, b:b + 1], place[b][0], AxisListType.X, OP.min, apply_absolute_value=True)],
+                                [place[b][1]], [("dd", b, b + 1)], max(64, 16 * b + 17) * CY)
+        at["cut"] = vts(xc, pd, 32.0, OP.min, 128, -32.0, OP.max)
+        at["list"] = vcp(msg(0, 8), o("dd", 0, 8), 8)
+        at["put"] = add("V", "c", [lambda: V.tensor_tensor(slot(r)[0].indirect(msg(0, 8)[0]), xo[0], xc[0], OP.add)], [xo[1], xc[1], msg(0, 8)[1]], [slot(r)[1]], 50 + 128 * SC * CY)
         if t < ROUNDS - 1:
             mm([(px, IDN, xo, 128), (px, IDN, xc, 128)])
-            vcp(msg(8, 136), px, 128)
+            at["new"] = vcp(msg(8, 136), px, 128)
 
     def send(t):
         m = o("inb%d" % t, r * MS, r * MS + MS)
@@ -470,7 +494,7 @@ def build(g, r, T, topo):
         q = (r + a) % N
         inb = "inb%d" % t
         x = T[inb]
-        w = 8 // TP
+        w = 8 // (TP if a > 1 else T1)
         name = slot(q)[1][0]
         before, done = list(hist[name]), []
         for j in range(0, 8, w):
@@ -494,14 +518,12 @@ def build(g, r, T, topo):
             late[1] = AHEAD * (1 - h)
             heads(t, h)
             late[1] = 0.0
-        if t:
-            book(t - 1)
         slots, takes = [], {}
         for a in range(N):
             if t and a:
                 for j, i in enumerate(take(t - 1, a)):
                     if a > 1:
-                        takes.setdefault(2 * a - 2 + 2 * j // TP if TP > 1 else 2 * a - 1, []).append(i)
+                        takes.setdefault(2 * a - 2 + 2 * j // TP, []).append(i)
             for h in range(2):
                 late[1] = AHEAD * (1 - h)
                 slots.append(visit(t, a, h))
@@ -516,10 +538,22 @@ def build(g, r, T, topo):
             if a == 0 and t < ROUNDS - 1:
                 spread(t + 1)
             if a == 1:
-                shares(t, 0, 1)
+                if t:
+                    book(t - 1)
+                    ops[-2]["d"].setdefault(slots[1]["vk"], False)
+                shares(t, takes)
                 keys(t)
+                if t:
+                    for row in BETWEEN:
+                        chain(row)
             late[0] = False
         weave(slots, takes)
+        at.clear()
+        at.update(turns)
+        at["vk1"] = slots[-1]["vk"]
+        for h in range(2):
+            for n, i in zip(("scan", "max", "and", "end"), slots[h - 2]["small"]):
+                at[n + str(h)] = i
         rows()
         elect(t)
         won(t)
@@ -528,6 +562,8 @@ def build(g, r, T, topo):
             kappa(t)
             send(t)
     book(ROUNDS - 1)
+    for row in LAST:
+        chain(row)
     dma("S", "yl", T.yl[:], note(r)[0], [note(r)[1]], [("yl", 0, 1)], 5500.0)
     return ops
 
@@ -586,7 +622,7 @@ def order(ops):
         free[e] = t0 + (60.0 if x["k"] == "d" else x["t"])
         seq.append(i)
         for j in succ[i]:
-            avail[j] = max(avail[j], end + (hop if ops[j]["d"][i] else 0.0))
+            avail[j] = max(avail[j], end + hop if ops[j]["d"][i] else free[e])
             missing[j] -= 1
             if not missing[j]:
                 ready.setdefault(ops[j]["e"], []).append(j)

from concourse.bass import DstId, RemoteDMATransfer
from concourse.mybir import AluOpType as OP, AxisListType, ActivationFunctionType as AF

N = 8
H, P0, B, ROUNDS = 4096, 1536, 128, 4
SL = B + H
W = 613 + 4096 * 228
R = (9 * W // 4096) * 4096
KAP0 = -8.0 - 13.0 / 32
BIG = 2.0 ** 18
MS = 144
E = 136
CT = [8 * b * (b + 1) + b for b in range(9)]
CUT = 5

SPLIT = {0: ((46,), 18), 15: ((50,), 14), "else": ((22, 8, 8), 14)}
AORD = ("ga0", "ga1", "sq", "sg0", "sg1", "vk")
SH = ("VVVA", "AAAV", "AAAV", "AAAV")
SW = (512, 512, 512, 256)
BETWEEN = ("max0 sv0 and0 scan1 end0 max1 end1 sv1", "X lo Y loff ks hv00 ki r7 r6 r5 kj cut r4 r3 r2 r1 r0 km list new hv10 put off0 cc0 hv11",
           "vk1 sg0 sg1 sr0 sg2 sr1 hi hw xo ha0 ha1", "sp0 rot01 rot18 step key8 sp1", "ev turn sum x5 y5 x0 y0 pd")
LAST = ("X Y loff r7 r6 r5 lo r4 r3 r2 r1 r0 list cut put", "ev x5 y5 x0 y0 pd turn")
SLACK = (150.0, 450.0)
EARLY = 3000.0
TP, T1 = 4, 1
FV = 0
AHEAD = 1500.0
HV = (((32,), (32,)), ((8,), (12,)))

SCRATCH = {"notes": ("sbuf", [128, N * SL], "bfloat16")}
for _d, _l in (("bfloat16", (("fe", 2048), ("hw", 2048), ("cnt", 2048), ("F0", 2048), ("F1", 2048), ("cs", 2048), ("gs", 1024), ("hdb", 192),
                             ("dm", 128), ("dmp", 128), ("blk", 128), ("nblk", 8), ("vv", 128), ("vt", 128), ("idn", 128), ("idm", 128), ("idb", 128),
                             ("ones", 128), ("xo", 128), ("xc", 128), ("hl", 128), ("rv", 128), ("rot", 1024), ("ee", 1024), ("xb", 1024),
                             ("jc", E), ("gcol", E), ("ofb", E), ("za", E), ("zb", E), ("zm", E), ("zr", E), ("rs", 8 * E), ("dp", E), ("dn", E),
                             ("d0", 2 * E), ("nr", 2 * E), ("zer", E), ("pen", 16), ("c21", 8), ("ct", CT[8]))),
               ("float16", (("c16", 128), ("xy", 256))),
               ("int32", (("ci0", 512), ("hdi", 96), ("hdx", 192), ("ia", 128), ("ib", 128), ("ja", 128), ("jb", 128), ("ka", 128), ("kb", 128),
                          ("iu", 128), ("iz", E), ("ix", 8), ("ki", 1), ("kj", 1))),
               ("uint16", (("offx", 8), ("loff", 8), ("offc", 128 * ROUNDS))),
               ("float32", (("col", 8), ("con", 8), ("run", 2 * E), ("er", 2 * E), ("dd", 8), ("d1", 8), ("ks", 1), ("kw", 128), ("yhs", 512),
                            ("kown", 8)))):
    for _n, _w in _l:
        SCRATCH[_n] = ("sbuf", [128, _w], _d)
for _h in range(2):
    for _n, _w, _d in (("gx", 1024, "bfloat16"), ("cm", 1024, "bfloat16"), ("off", 64, "uint16"), ("ci", 64, "int32"), ("cc", 64, "float32"),
                       ("sq", 64, "float32"), ("vs", 64, "float32"), ("qi", 64, "int32")):
        SCRATCH[_n + "_%d" % _h] = ("sbuf", [128, _w], _d)
    SCRATCH["vk_%d" % _h] = ("sbuf", [128, 128], "float32")
    for _n in ("nn", "df", "fp"):
        SCRATCH[_n + "_%d" % _h] = ("psum", [128, 512], "float32")
for _n in ("sh", "key"):
    SCRATCH[_n] = ("psum", [128, 512], "float32")
for _t in range(ROUNDS):
    SCRATCH["inb%d" % _t] = ("sbuf", [128, N * MS], "uint16")
    SCRATCH["kap%d" % _t] = ("sbuf", [128, N], "float32")

DMAS = ["comp0", "comp1", "hd", "fe0", "fe1", "lim", "hwa", "hwb", "yh0", "yh1", "yh2", "yh3", "yl"]
SEMAPHORES = (["pV", "pA", "pP", "pG", "lsem", "msem"] + ["d_" + n for n in DMAS] + ["lim%d" % q for q in range(N)]
              + ["m%d_%d" % (t, q) for t in range(ROUNDS - 1) for q in range(N)])

TIMES = {"cy": 0.95, "pe": 0.5, "hop": 210.0, "gather": 1.5, "scatter": 3.5, "note": 3700.0}


def build(g, r, T, topo):
    ops = []
    hist = {}
    banks = {}
    at, turns = {}, {}
    core = T.cores[r]
    V, A, PE, S = g.vector, g.scalar, g.tensor, g.sync
    CY, PC, GA, SC = (TIMES[n] for n in ("cy", "pe", "gather", "scatter"))
    late = [False, 0.0]

    def add(eng, kind, fns, reads, writes, dur, name=None, extra=()):
        i = len(ops)
        deps = {}
        for u in extra:
            deps[u] = True
        for buf, lo, hi in reads:
            for acc in hist.get(buf, ()):
                if acc[3] and acc[1] < hi and lo < acc[2]:
                    deps[acc[0]] = True
        for buf, lo, hi in writes:
            for acc in hist.get(buf, ()):
                if acc[1] < hi and lo < acc[2]:
                    deps[acc[0]] = deps.get(acc[0], False) or eng != "P" or ops[acc[0]]["e"] != "P"
        for buf in sorted({x[0] for x in list(reads) + list(writes)}):
            if SCRATCH.get(buf, ("",))[0] == "psum":
                last = banks.setdefault(buf, {})
                for e, u in last.items():
                    if e != eng:
                        deps[u] = True
                    else:
                        deps.setdefault(u, False)
                last[eng] = i
        for buf, lo, hi in writes:
            h = [a for a in hist.get(buf, []) if not (lo <= a[1] and a[2] <= hi)]
            h.append((i, lo, hi, True))
            hist[buf] = h
        for buf, lo, hi in reads:
            hist.setdefault(buf, []).append((i, lo, hi, False))
        deps.pop(i, None)
        ops.append({"e": eng, "k": kind, "f": fns, "d": deps, "t": dur, "n": name, "late": late[0], "u": late[1]})
        return i

    def o(name, lo, hi, step=1):
        return (T[name][:, lo:hi:step] if step > 1 else T[name][:, lo:hi], (name, lo, hi))

    def narrow(*xs):
        return 0.5 if all(SCRATCH[x[1][0]][2] in ("bfloat16", "float16", "uint16") for x in xs) else 1.0

    def vtt(out, a, b, op, n):
        both = all(SCRATCH[x[1][0]][0] == "sbuf" for x in (a, b))
        return add("V", "c", [lambda: V.tensor_tensor(out[0], a[0], b[0], op)], [a[1], b[1]], [out[1]], max(64, n * (2 if both else 1)) * CY)

    def vts(out, a, s1, op, n, s2=None, op1=None):
        col = isinstance(s1, tuple)
        x = s1[0] if col else s1

        def f():
            if op1 is None:
                return V.tensor_scalar(out[0], a[0], x, None, op)
            return V.tensor_scalar(out[0], a[0], x, s2, op, op1)
        return add("V", "c", [f], [a[1]] + ([s1[1]] if col else []), [out[1]], max(64, n * narrow(out, a)) * CY)

    def vcp(out, a, n):
        return add("V", "c", [lambda: V.tensor_copy(out[0], a[0])], [a[1]], [out[1]], max(64, n * narrow(out, a)) * CY)

    def scan(out, a, b, op0, op1, n):
        return add("V", "c", [lambda: V.tensor_tensor_scan(out[0], a[0], b[0], 0.0, op0, op1)], [a[1], b[1]], [out[1]], max(64, n) * CY)

    def fill(x, v, n=64):
        return add("V", "c", [lambda: V.memset(x[0], v)], [], [x[1]], max(64, n * narrow(x)) * CY)

    def act(out, a, n, func=AF.Copy, bias=None, scale=None, acc=None):
        kw = {}
        if bias:
            kw["bias"] = bias[0]
        if scale:
            kw["scale"] = scale
        if acc:
            kw["accum_out"] = acc[0]
        return add("A", "c", [lambda: A.activation(out[0], a[0], func, **kw)], [a[1]] + ([bias[1]] if bias else []),
                   [out[1]] + ([acc[1]] if acc else []), 65 + n * CY)

    def agather(out, win, offs, n):
        return add("A", "c", [lambda: A.activation(out[0], win[0].indirect(offs[0]), AF.Copy)], [win[1], offs[1]], [out[1]], 65 + n * GA * CY)

    def vgather(out, win, offs, n):
        return add("V", "c", [lambda: V.tensor_copy(out[0], win[0].indirect(offs[0]))], [win[1], offs[1]], [out[1]], 50 + n * GA * CY)

    def vgtt(out, win, offs, b, op, n):
        return add("V", "c", [lambda: V.tensor_tensor(out[0], win[0].indirect(offs[0]), b[0], op)], [win[1], offs[1], b[1]], [out[1]], 50 + n * GA * CY)

    def mm(steps, first=True, last=True, again=False):
        k = len(steps) - 1
        fns = [(lambda s=s, i=i: PE.matmul(s[0][0], s[1][0], s[2][0], first and i == 0, last and i == k)) for i, s in enumerate(steps)]
        outs = sorted({s[0][1] for s in steps})
        return add("P", "c", fns, sorted({x[1] for s in steps for x in s[1:3]}), outs, sum(max(64, s[3]) for s in steps) * PC * CY)

    def dma(q, name, out, in_, reads, writes, dur=2500.0):
        eng = {"S": S, "A": A}[q]
        return add(q, "d", [lambda: eng.dma_start(out, in_)], reads, writes, dur, name)

    def cnt(a):
        return o("cnt", 128 * a, 128 * a + 128)

    def count(out, buf):
        return mm([(out, cnt(a), (T[buf][:, a:1024:16], (buf, 0, 1024)), 64) for a in range(16)])

    w128 = lambda n: o(n, 0, 128)
    IDN, IDM, IDB, BLK = w128("idn"), w128("idm"), w128("idb"), w128("blk")
    con = lambda i: o("con", i, i + 1)
    note = lambda q: o("notes", q * SL + B, q * SL + SL)
    slot = lambda q: o("notes", q * SL, q * SL + SL)
    goods = lambda t: o("fe", P0 + 128 * t, P0 + 128 * t + 128)

    dma("A", "lim", note(r)[0], T.lim[:], [], [note(r)[1]], 5500.0)
    dma("S", "hd", T.hdi[:], T.hd[:], [], [("hdi", 0, 96)])
    dma("S", "comp0", T.ci0[:, 0:128], T.comp[:, 0:128], [], [("ci0", 0, 128)])
    dma("S", "fe1", T.fe[:, P0:2048], T.feat[:, P0:2048], [], [("fe", P0, 2048)], 3000.0)

    def iota(name, w, pat, base, ch):
        out = T[name]
        kw = {} if SCRATCH[name][2] == "int32" else {"allow_small_or_imprecise_dtypes": True}
        add("G", "c", [lambda: g.iota(out[:, 0:w], pat, base, ch, **kw)], [], [(name, 0, w)], 130 + 2 * w * CY)

    def select(out, a, pat, base, ch, n):
        add("G", "c", [lambda: g.affine_select(out[0], a[0], pat, OP.is_ge, 0.0, base, ch)], [a[1]], [out[1]], 170 + 2 * n * CY)
    iota("ia", 128, [[0, 128]], 0, 1)
    iota("ib", 128, [[1, 128]], 0, 0)
    iota("iu", 128, [[-1, 128]], 128, 1)
    iota("iz", E, [[0, 8], [1, 17]], 1, 1)
    iota("jc", E, [[0, 8], [1, 17]], 0, 0)
    iota("gcol", E, [[1, 8], [0, 17]], 0, 0)
    iota("ix", 8, [[17, 8]], E + 16, 0)
    zeros = fill(o("hw", 0, 2048), 0.0, 2048)
    for i, v in enumerate((16.0 - R, float(R), -100.0, KAP0)):
        fill(con(i), v)
    vts(o("hdx", 0, 96), o("hdi", 0, 96), 4032, OP.bitwise_and, 96)
    vts(o("hdx", 96, 192), o("hdi", 0, 96), 63, OP.bitwise_and, 96)
    vcp(o("hdb", 0, 192), o("hdx", 0, 192), 192)
    dma("S", "hwa", T.hw[0:128:16, 0:P0], T.hdb[:, 0:96], [("hdb", 0, 96)], [("hw", 0, P0)])
    keep = list(hist["hw"])
    hist["hw"] = []
    i2 = dma("S", "hwb", T.hw[1:128:16, 0:P0], T.hdb[:, 96:192], [("hdb", 96, 192)], [("hw", 0, P0)])
    ops[i2]["d"][zeros] = True
    hist["hw"] = keep + [(i2, 0, P0, True)]
    i3 = dma("S", "fe0", T.fe[:, 0:P0], T.feat[:, 0:P0], [], [("fe", 0, P0)], 4000.0)
    i4 = dma("S", "comp1", T.ci0[:, 128:512], T.comp[:, 128:512], [], [("ci0", 128, 512)], 4000.0)
    ops[i3]["d"][i2] = ops[i4]["d"][i3] = False
    vts(w128("ja"), w128("ia"), 4, OP.arith_shift_right, 128)
    vts(w128("jb"), w128("ib"), 4, OP.arith_shift_right, 128)
    vts(w128("ka"), w128("ia"), 15, OP.bitwise_and, 128)
    vts(w128("kb"), w128("ib"), 15, OP.bitwise_and, 128)
    vtt(BLK, w128("ja"), w128("jb"), OP.is_equal, 128)
    vts(w128("vt"), BLK, -99.0, OP.mult, 128, 99.0, OP.add)
    vtt(w128("vv"), w128("vt"), w128("kb"), OP.add, 128)
    for a in range(16):
        vts(cnt(a), w128("vv"), float(a), OP.is_equal, 128)
    vtt(IDN, w128("ia"), w128("ib"), OP.is_equal, 128)
    vts(IDM, IDN, -1.0, OP.mult, 128)
    vcp(o("offc", 0, 128), o("ci0", 0, 128), 128)

    def spread(t):
        name = "F%d" % (t % 2)
        keep = [x for x in hist.get(name, [])]
        done = []
        for k in range(16):
            hist[name] = list(keep)
            out = (T[name][:, k:2048:16], (name, 0, 2048))
            if t == 0 and k < FV:
                vcp(out, goods(t), 128)
            elif t == 0:
                act(out, goods(t), 128)
            else:
                select(out, goods(t), [[0, 128]], 0, 0, 128)
            done.append((len(ops) - 1, 0, 2048, True))
        hist[name] = done
    spread(0)

    for a in range(1, N):
        dst = T.cores[(r - a) % N]

        def fn(dst=dst):
            rid, pid = topo.addr(dst)[:2]
            return g.remote_dma(note(r)[0], note(r)[0], T.sem["lim%d" % r], T.sem.lsem, pid, rid, topo.mask(core, dst))
        sent = add("G", "r", [fn], [note(r)[1]], [], 1000.0, name=("lsem", len(topo.engines(core, dst))))
        q = (r + a) % N
        add("X", "a", [], [], [note(q)[1]], 1000.0 + (TIMES["note"] - 1000.0) * a, ("lim%d" % q, len(topo.engines(T.cores[q], core))), extra=[sent])

    def tables():
        e = lambda n: o(n, 0, E)
        col = lambda i: o("col", i, i + 1)
        vcp(o("offc", 128, 512), o("ci0", 128, 512), 384)
        fill(e("zer"), 0.0)
        vts(o("nblk", 0, 8), o("blk", 0, 128, 16), -1.0, OP.mult, 8)
        vtt(w128("dm"), w128("ka"), w128("kb"), OP.is_equal, 128)
        vcp(col(0), o("ja", 0, 1), 1)
        vts(col(1), o("ka", 0, 1), 1.0, OP.add, 1)
        vts(col(2), o("ia", 0, 1), 1.0 / 8192, OP.mult, 1)
        vts(w128("dmp"), w128("dm"), col(2), OP.mult, 128)
        vts(IDB, IDN, -8192.0, OP.mult, 128)
        fill(w128("ones"), 1.0)
        fill(w128("hl"), 0.0)
        fill(o("hl", 2, 128, 16), 2048.0)
        vcp(o("offx", 0, 8), o("ix", 0, 8), 8)
        vcp(col(3), o("ka", 0, 1), 1)
        vts(o("pen", 0, 16), o("jc", 0, 16), col(3), OP.is_ge, 16, -8192.0, OP.mult)
        vts(w128("iu"), w128("iu"), 15, OP.bitwise_and, 128)
        vtt(w128("rv"), w128("iu"), w128("vt"), OP.add, 128)
        for s in range(1, 9):
            vts(o("rot", 128 * s - 128, 128 * s), w128("rv"), float(s), OP.is_equal, 128)
        vts(e("ofb"), e("gcol"), col(0), OP.not_equal, E, 99.0, OP.mult)
        vts(e("za"), e("jc"), col(1), OP.add, E)
        vtt(e("zm"), e("za"), e("ofb"), OP.add, E)
        vts(e("dp"), e("zm"), 17.0, OP.is_equal, E)
        vts(e("dn"), e("zm"), 16.0, OP.is_equal, E, -1.0, OP.mult)
        vts(e("iz"), e("iz"), 15, OP.bitwise_and, E)
        vts(e("za"), e("jc"), 16.0, OP.is_equal, E, 50.0, OP.mult)
        vtt(e("zb"), e("za"), e("ofb"), OP.add, E)
        vtt(e("zr"), e("zb"), e("iz"), OP.add, E)
        for s in range(8):
            vts(o("rs", E * s, E * s + E), e("zr"), float((16 - s) % 16), OP.is_equal, E, 4096.0, OP.mult)
        fill(o("d0", 0, 2 * E), 0.0, 2 * E)
        for w, sign in enumerate((1.0, -1.0)):
            fill(o("d0", E * w, E * w + E, 17), -3 * BIG * sign)
            fill(o("d0", E * w + 16, E * w + E, 17), BIG * sign)
        xb = o("xb", 0, 1024)
        iota("xb", 1024, [[0, 1024]], 8192, 0)
        ops[-1]["d"][sent] = False
        select(xb, xb, [[-16, 8], [0, 128]], 0, 1, 1024)
        select(xb, xb, [[16, 8], [0, 128]], 15, -1, 1024)
        for s in range(1, 8):
            x = o("key", 0, E)
            mm([(x, IDN, o("rs", E * s, E * s + E), E), (x, IDN, o("rs", 0, E), E)])
            act(o("rs", E * s, E * s + E), x, E)
        fill(o("ct", 0, CT[8]), 2048.0 + B, CT[8])
        for b in range(8):
            w, c = 16 * b + 16, CT[b]
            x = o("key", 0, w)
            mm([(x, w128("dmp"), o("xb", 128 * b, 128 * b + w), w), (o("key", w - 16, w), IDB, o("pen", 0, 16), 16)])
            act(o("ct", c, c + w), x, w)

    def heads(t, h):
        oc = 128 * t + 64 * h
        gx, hw = "gx_%d" % h, o("hw", 0, 2048)
        cv = 0
        for j, w in enumerate(HV[min(t, 1)][h]):
            at["hv%d%d" % (h, j)] = vgather(o(gx, 16 * cv, 16 * (cv + w)), hw, o("offc", oc + cv, oc + cv + w), 16 * w)
            cv += w
        at["ha%d" % h] = agather(o(gx, 16 * cv, 1024), hw, o("offc", oc + cv, oc + 64), 1024 - 16 * cv)
        out = o("nn_%d" % h, 0, 64)
        count(out, gx)
        at["off%d" % h] = vcp(o("off_%d" % h, 0, 64), out, 64)
        at["cc%d" % h] = vts(o("cc_%d" % h, 0, 64), out, float(R), OP.add, 64)

    def shares(t, takes):
        F = "F%d" % (t % 2)
        fe = o("fe", 0, 2048)
        offs = lambda c, w: o("offc", 128 * t + c // 16, 128 * t + (c + w) // 16)
        for j in range(4):
            w = (128 if SH[t][j] == "V" else 256) if t == 0 else SW[j]
            for c in range(512 * j, 512 * j + 512, w):
                if SH[t][j] == "V":
                    i = at["sv%d" % (c // w % 2)] = vgtt(o("cs", c, c + w), fe, offs(c, w), o(F, c, c + w), OP.min, w)
                    if t == 0:
                        takes[len(takes) + 2] = [i]
                    continue
                gs, d = o("gs", c % 1024, c % 1024 + w), o("sh", 0, w)
                at["sg%d" % j] = agather(gs, fe, offs(c, w), w)
                at["sp%d" % j] = mm([(d, IDN, o(F, c, c + w), w), (d, IDM, gs, w)])
                at["sr%d" % j] = act(o("cs", c, c + w), d, w, AF.Relu)

    def chain(names):
        lst = [at[n] for n in names.split() if n in at]
        for u, i in zip(lst, lst[1:]):
            ops[i]["d"].setdefault(u, False)

    def keys(t):
        sign = {"V": o("blk", 0, 128, 16), "A": o("nblk", 0, 8)}
        mm([(o("key", 0, E), IDN, o("zer", 0, E), E)], last=False)
        cuts = [0] + [32 * j for j in range(1, 4) if SH[t][j] != SH[t][j - 1]] + [128]
        for lo, hi in zip(cuts, cuts[1:]):
            for k0 in range(0, 16, 4):
                mm([((T.key[lo:hi, 15 - k:E:17], ("key", 0, E)), (T.cs[:, 16 * lo + k:16 * hi:16], ("cs", 16 * lo, 16 * hi)), sign[SH[t][lo // 32]], 8)
                    for k in range(k0, k0 + 4)], first=False, last=False)

    def visit(t, a, h):
        q = (r + a) % N
        nm = lambda n: n + "_%d" % h
        s64 = lambda n: o(nm(n), 0, 64)
        F, f0 = "F%d" % (t % 2), 1024 * h
        CV, CA = SPLIT.get(2 * a + h, SPLIT["else"])
        cv = sum(CV)
        x = {}
        for j, bank, lo, hi in ((0, "df", cv, cv + CA), (1, "fp", cv + CA, 64)):
            w = 16 * (hi - lo)
            if w:
                d, gx = o(nm(bank), 0, w), o(nm("gx"), 16 * lo, 16 * hi)
                mm([(d, IDN, o(F, f0 + 16 * lo, f0 + 16 * hi), w)], last=False)
                x["ga%d" % j] = agather(gx, note(q), o(nm("off"), lo, hi), w)
                mm([(d, IDM, gx, w)], first=False)
                x["sg%d" % j] = act(o(nm("cm"), 16 * lo, 16 * hi), d, w, AF.Sigmoid, con(2), 200.0)
        cuts = [sum(CV[:i]) for i in range(len(CV) + 1)]
        x["gv"] = [vgtt(o(nm("cm"), 16 * lo, 16 * hi), note(q), o(nm("off"), lo, hi), o(F, f0 + 16 * lo, f0 + 16 * hi), OP.is_lt, 16 * (hi - lo))
                   for lo, hi in zip(cuts, cuts[1:])]
        x["sq"] = act(s64("sq"), s64("cc"), 64, AF.Square, con(0))
        kap = con(3) if t == 0 else o("kown", t, t + 1) if a == 0 else o("kap%d" % t, q, q + 1)
        x["vk"] = act(o(nm("vk"), 1, 128, 2), s64("sq"), 64, AF.Identity, kap, 1.0 / 32)
        count(o(nm("nn"), 385, 512, 2), nm("cm"))
        x["small"] = [scan(o(nm("nn"), 128, 256), o(nm("nn"), 384, 512), o(nm("vk"), 0, 128), OP.mult, OP.add, 128),
                      vtt(s64("qi"), o(nm("nn"), 129, 256, 2), s64("cc"), OP.max, 64),
                      vts(s64("ci"), s64("qi"), 4095, OP.bitwise_and, 64)]
        if a < N - 1:
            x["small"].append(vcp(s64("off"), s64("ci"), 64))
            x["cc"] = [vts(s64("cc"), s64("ci"), float(R), OP.add, 64)]
        else:
            x["small"].append(vts(o("c16", 64 * h, 64 * h + 64), s64("ci"), -2048.0, OP.add, 64))
        return x

    def weave(slots, takes):
        row = []
        for s, x in enumerate(slots):
            row += slots[s - 2]["cc"] if s > 1 else []
            fill_ = [[i] for i in x["gv"]]
            extra = takes.get(s, [])
            row += extra[:-1]
            fill_ += [[]] * (3 - len(fill_)) + [extra[-1:]]
            for j in range(4):
                row += fill_[j] + (slots[s - 1]["small"][j:j + 1] if s else [])
        rows_ = [row, [x[n] for x in slots for n in AORD if n in x]]
        for lst in rows_:
            for u, i in zip(lst, lst[1:]):
                ops[i]["d"].setdefault(u, False)

    def pairs(h):
        c = o("c16", 64 * h, 64 * h + 64)
        for bank, lst in (("df_%d" % h, (1, 2, 3)), ("nn_%d" % h, (4, 5, 6, 7, 8))):
            place = lambda s: o(bank, 64 * (s - lst[0]), 64 * (s - lst[0]) + 64)
            for s in lst:
                turns["rot%d%d" % (h, s)] = mm([(place(s), o("rot", 128 * s - 128, 128 * s), c, 64)])
            for s in lst:
                turns["eq%d%d" % (h, s)] = vtt(o("ee", 128 * s - 128 + 64 * h, 128 * s - 64 + 64 * h), place(s), c, OP.is_equal, 64)

    def elect(t):
        key, dl = o("key", 0, E), o("nn_0", 0, E)
        at["step"] = mm([(dl, w128("c16"), o("dp", 0, E), E), (dl, w128("c16"), o("dn", 0, E), E)])
        for s in range(1, 9):
            ee = o("ee", 128 * s - 128, 128 * s)
            at["key%d" % s] = mm([(key, ee, o("rs", E * (s % 8), E * (s % 8) + E), E)], first=False, last=s == 8)
        half = lambda n, w: o(n, E * w, E * w + E)
        for w, op in enumerate((OP.max, OP.min)):
            scan(half("run", w), half("d0", w), key, OP.add, op, E)
        for w in range(2):
            vtt(half("nr", w), key, half("run", w), OP.not_equal, E)
        for w in range(2):
            scan(half("er", w), dl, half("nr", w), OP.add, OP.mult, E)

    def won(t):
        v, hi, lo = o("er", 16, E, 17), o("hl", 0, 128, 16), o("hl", 1, 128, 16)
        at["hi"] = act(hi, v, 8)
        at["lo"] = vtt(lo, v, hi, OP.subtract, 8)
        x = o("df_0", 0, 128)
        at["turn"] = mm([(x, w128("hl"), IDN, 128)])
        at["hw"] = act(o("hw", P0 + 128 * t, P0 + 128 * t + 128), x, 128)

    def book(t):
        x = o("key", 256, 384)
        mm([(x, BLK, o("hw", P0 + 128 * t, P0 + 128 * t + 128), 128)])
        act(o("yhs", 128 * t, 128 * t + 128), x, 128)
        dma("S", "yh%d" % t, T.yh[:, 128 * t:128 * t + 128], T.yhs[0:128:16, 128 * t:128 * t + 128], [("yhs", 128 * t, 128 * t + 128)], [("yh", 128 * t, 128 * t + 128)])

    def kappa(t):
        x = o("key", 256, 384)
        ks, ki, kj = o("ks", 0, 1), o("ki", 0, 1), o("kj", 0, 1)
        at["sum"] = mm([(x, w128("ones"), w128("hl"), 128)])
        at["ks"] = add("V", "c", [lambda: V.tensor_reduce(ks[0], x[0], AxisListType.X, OP.add)], [x[1]], [ks[1]], 128 * CY)
        at["ki"] = vcp(ki, ks, 1)
        at["kj"] = vts(kj, ki, 255, OP.bitwise_and, 1)
        vts(o("kown", t + 1, t + 2), kj, KAP0, OP.add, 1)
        at["km"] = vcp(o("inb%d" % t, r * MS + 136, r * MS + 137), kj, 1)

    def rows():
        for bank, lo, hi in (("fp_0", 0, CT[CUT]), ("fp_1", CT[CUT], CT[8])):
            mm([(o(bank, 0, hi - lo), IDN, o("ct", lo, hi), hi - lo)], last=False)

    def lost(t):
        er, ox = o("er", 0, 2 * E), o("offx", 0, 8)
        X, Y = o("xy", 0, 128), o("xy", 128, 256)
        msg = lambda lo, hi: o("inb%d" % t, r * MS + lo, r * MS + hi)
        at["X"] = vgtt(X, er, ox, w128("dm"), OP.mult, 128)
        at["Y"] = vgather(Y, er, ox, 128)
        ev = o("nn_1", 256, 264)
        at["ev"] = mm([(ev, X, o("blk", 0, 128, 16), 8)])
        at["loff"] = vts(o("loff", 0, 8), ev, 2048.0, OP.add, 8)
        part = lambda b, lo, hi: o("fp_%d" % (b >= CUT), CT[b] - CT[CUT] * (b >= CUT) + lo, CT[b] - CT[CUT] * (b >= CUT) + hi)
        place = [part(b, 0, 16 * b + 17) for b in range(8)]
        banks_ = (range(CUT, 8), range(CUT))
        for bs in banks_:
            at["x%d" % bs[0]] = mm([(part(b, 0, 16 * b + 16), X, o("xb", 128 * b, 128 * b + 16 * b + 16), 16 * b + 16) for b in bs]
                                   + [(part(b, 16 * b + 16, 16 * b + 17), X, o("blk", 16 * b, 16 * b + 1), 1) for b in bs], first=False, last=False)
            at["y%d" % bs[0]] = mm([(part(b, 0, 16 * b + 16), Y, o("idb", 0, 16 * b + 16), 16 * b + 16) for b in bs], first=False)
        xo, xc = w128("xo"), w128("xc")
        at["xo"] = agather(xo, note(r), o("loff", 0, 8), 128)
        pd, px = o("df_1", 0, 128), o("df_1", 128, 256)
        at["pd"] = mm([(pd, IDN, goods(t), 128), (pd, IDM, xo, 128)])
        for b in reversed(range(8)):
            at["r%d" % b] = add("V", "c", [lambda b=b: V.tensor_reduce(T.dd[:, b:b + 1], place[b][0], AxisListType.X, OP.min, apply_absolute_value=True)],
                                [place[b][1]], [("dd", b, b + 1)], max(64, 16 * b + 17) * CY)
        at["cut"] = vts(xc, pd, 32.0, OP.min, 128, -32.0, OP.max)
        at["list"] = vcp(msg(0, 8), o("dd", 0, 8), 8)
        at["put"] = add("V", "c", [lambda: V.tensor_tensor(slot(r)[0].indirect(msg(0, 8)[0]), xo[0], xc[0], OP.add)], [xo[1], xc[1], msg(0, 8)[1]], [slot(r)[1]], 50 + 128 * SC * CY)
        if t < ROUNDS - 1:
            mm([(px, IDN, xo, 128), (px, IDN, xc, 128)])
            at["new"] = vcp(msg(8, 136), px, 128)

    def send(t):
        m = o("inb%d" % t, r * MS, r * MS + MS)
        others = [T.cores[(r - a) % N] for a in range(1, N)]
        mask = topo.mask(core, others[0])

        def fn():
            ids = [DstId(rid=topo.addr(c)[0], pnc=topo.addr(c)[1]) for c in others]
            return g.remote_dma_fused([RemoteDMATransfer(dst_ids=ids, dma_engine_mask=mask, remote_sem=T.sem["m%d_%d" % (t, r)],
                                                         srcs=[m[0]], dsts=[m[0] for c in ids], alu_op=0)], local_sem=T.sem.msem)
        ne = len(topo.engines(core, others[0]))
        s = add("G", "r", [fn], [m[1]], [], 1000.0, name=("msem", ne))
        for a in range(1, N):
            q = (r + a) % N
            add("X", "a", [], [], [("inb%d" % t, q * MS, q * MS + MS)], 2500.0, ("m%d_%d" % (t, q), ne), extra=[s])

    def take(t, a):
        q = (r + a) % N
        inb = "inb%d" % t
        x = T[inb]
        w = 8 // (TP if a > 1 else T1)
        name = slot(q)[1][0]
        before, done = list(hist[name]), []
        for j in range(0, 8, w):
            hist[name] = list(before)
            c = q * MS + 8 + 16 * j
            i = add("V", "c", [lambda j=j, c=c: V.tensor_copy(slot(q)[0].indirect(x[:, q * MS + j:q * MS + j + w]), x[:, c:c + 16 * w])],
                    [(inb, q * MS, q * MS + MS)], [slot(q)[1]], 50 + 16 * w * SC * CY)
            if done:
                ops[i]["d"][done[-1][0]] = True
            done.append((i, q * SL, q * SL + SL, True))
        hist[name] = [z for z in hist[name] if z[0] != done[-1][0]] + done
        if a == 1:
            vts(o("kap%d" % (t + 1), 0, N), (x[:, 136:N * MS:MS], (inb, 0, N * MS)), KAP0, OP.add, N)
        return [z[0] for z in done]

    for t in range(ROUNDS):
        for h in range(2):
            if t == 0:
                fill(o("nn_%d" % h, 384, 512), 0.0, 128)
                fill(o("vk_%d" % h, 0, 128), float(W), 128)
            late[1] = AHEAD * (1 - h)
            heads(t, h)
            late[1] = 0.0
        slots, takes = [], {}
        for a in range(N):
            if t and a:
                for j, i in enumerate(take(t - 1, a)):
                    if a > 1:
                        takes.setdefault(2 * a - 2 + 2 * j // TP, []).append(i)
            for h in range(2):
                late[1] = AHEAD * (1 - h)
                slots.append(visit(t, a, h))
                late[1] = 0.0
                if a == N - 1:
                    pairs(h)
            late[0] = True
            if t == 0 and a == 0:
                tables()
                for u in range(ROUNDS - 1):
                    fill(o("inb%d" % u, r * MS + 137, r * MS + MS), 0)
            if a == 0 and t < ROUNDS - 1:
                spread(t + 1)
            if a == 1:
                if t:
                    book(t - 1)
                    ops[-2]["d"].setdefault(slots[1]["vk"], False)
                shares(t, takes)
                keys(t)
                if t:
                    for row in BETWEEN:
                        chain(row)
            late[0] = False
        weave(slots, takes)
        at.clear()
        at.update(turns)
        at["vk1"] = slots[-1]["vk"]
        for h in range(2):
            for n, i in zip(("scan", "max", "and", "end"), slots[h - 2]["small"]):
                at[n + str(h)] = i
        rows()
        elect(t)
        won(t)
        lost(t)
        if t < ROUNDS - 1:
            kappa(t)
            send(t)
    book(ROUNDS - 1)
    for row in LAST:
        chain(row)
    dma("S", "yl", T.yl[:], note(r)[0], [note(r)[1]], [("yl", 0, 1)], 5500.0)
    return ops


def order(ops):
    n = len(ops)
    hop = TIMES["hop"]
    succ = [[] for _ in range(n)]
    for i, x in enumerate(ops):
        for u in x["d"]:
            succ[u].append(i)
    left = [len(x["d"]) for x in ops]
    serial = [i for i in range(n) if not left[i]]
    for i in serial:
        for j in succ[i]:
            left[j] -= 1
            if not left[j]:
                serial.append(j)
    tail = [0.0] * n
    for i in reversed(serial):
        tail[i] = ops[i]["t"] + max([(hop if ops[j]["d"][i] else 0.0) + tail[j] for j in succ[i]] + [0.0])
    urge = lambda j: (tail[j] + ops[j]["u"] + (EARLY if ops[j]["late"] else 0.0), -j)
    missing = [len(x["d"]) for x in ops]
    avail = [0.0] * n
    ready = {}
    for i in range(n):
        if not missing[i]:
            ready.setdefault(ops[i]["e"], []).append(i)
    free = {}
    seq = []
    start = [0.0] * n
    while len(seq) < n:
        best = None
        for e, lst in ready.items():
            if not lst:
                continue
            f = 0.0 if e == "X" else free.get(e, 0.0)
            t0 = min(max(f, avail[i]) for i in lst)
            now = [j for j in lst if max(f, avail[j]) <= t0 + 1e-6]
            i = max(now, key=urge)
            soon = [j for j in lst if t0 < avail[j] <= t0 + SLACK[ops[i]["late"]] and urge(j) > urge(i)]
            if soon and e != "X":
                j = max(soon, key=urge)
                fit = [k for k in now if t0 + ops[k]["t"] <= avail[j] + 20]
                if fit:
                    i = max(fit, key=urge)
                else:
                    i, t0 = j, avail[j]
            if best is None or t0 < best[0]:
                best = (t0, i, e)
        t0, i, e = best
        ready[e].remove(i)
        x = ops[i]
        end = t0 + x["t"]
        start[i] = t0
        free[e] = t0 + (60.0 if x["k"] == "d" else x["t"])
        seq.append(i)
        for j in succ[i]:
            avail[j] = max(avail[j], end + hop if ops[j]["d"][i] else free[e])
            missing[j] -= 1
            if not missing[j]:
                ready.setdefault(ops[j]["e"], []).append(j)
    return seq, start


def rank_program(g, core, T, topo):
    r = T.rank_of(core)
    if r is None:
        return
    ops = build(g, r, T, topo)
    seq, _ = order(ops)
    queue = {"V": g.vector, "A": g.scalar, "P": g.tensor, "G": g, "S": g.sync}
    total = {}
    key = {}
    clock = {}
    known = {e: {} for e in queue}
    for i in seq:
        x = ops[i]
        e = x["e"]
        if x["k"] == "a":
            key[i] = x["n"]
            clock[i] = {x["n"][0]: x["n"][1]}
            total[x["n"][0]] = x["n"][1]
            continue
        kn = known[e]
        need = {}
        for u, raw in x["d"].items():
            if not raw:
                continue
            s, c = key[u]
            if kn.get(s, 0) < c:
                need.setdefault(s, []).append((c, u))
        for s in sorted(need, key=lambda z: -max(need[z])[1]):
            c, u = max(need[s])
            if kn.get(s, 0) < c:
                queue[e].wait_ge(T.sem[s], c)
                for a, b in clock[u].items():
                    kn[a] = max(kn.get(a, 0), b)
        if x["k"] == "c":
            s = "p" + e
            for f in x["f"]:
                f().then_inc(T.sem[s], 1)
                total[s] = total.get(s, 0) + 1
            key[i] = (s, total[s])
        elif x["k"] == "d":
            s = "d_" + x["n"]
            x["f"][0]().then_inc(T.sem[s], 16)
            total[s] = 16
            key[i] = (s, 16)
        else:
            x["f"][0]()
            s, c = x["n"]
            total[s] = total.get(s, 0) + c
            key[i] = (s, total[s])
        clock[i] = dict(kn)
        clock[i][key[i][0]] = key[i][1]
    for s in sorted(total):
        if known["G"].get(s, 0) < total[s]:
            g.wait_ge(T.sem[s], total[s])
